import numpy as np
import ml_dtypes


def mxq(x, axis, fmt="e4m3"):
    dtype, down = {"e4m3": (ml_dtypes.float8_e4m3fn, 7), "e5m2": (ml_dtypes.float8_e5m2, 14)}[fmt]
    v = np.moveaxis(np.asarray(x, np.float32).astype(ml_dtypes.bfloat16).astype(np.float64), axis, -1)
    blocks = v.reshape(v.shape[:-1] + (-1, 32))
    amax = np.abs(blocks).max(-1, keepdims=True)
    byte = np.maximum(np.where(amax > 0, np.frexp(amax)[1] - 1 + 127, 0) - down, 1)
    scale = np.exp2(byte - 127.0)
    codes = (blocks / scale).astype(np.float32).astype(dtype).astype(np.float64)
    return np.moveaxis((codes * scale).reshape(v.shape), -1, axis)


WIDE = False


def mx_kscale(k):
    if not WIDE:
        return np.ones(k)
    levels = np.array([10, -10, 5, -5, 0])
    if k % 512:
        return np.exp2(np.random.permutation(np.resize(levels, k // 32))).repeat(32)
    a = np.empty((k // 512, 16))
    for p in range(k // 512):
        a[p, :8] = np.random.permutation(np.resize(levels, 8))
        for g in range(8):
            far = levels[np.abs(levels - a[p, g]) >= 10]
            a[p, g + 8] = far[np.random.randint(len(far))]
    return np.exp2(a.ravel()).repeat(32)


BF16 = ml_dtypes.bfloat16


def bf(x):
    return np.asarray(x, np.float32).astype(BF16)


def f64(x):
    return np.asarray(x).astype(np.float64)


E2M1 = np.array([0.0, 0.5, 1.0, 1.5, 2.0, 3.0, 4.0, 6.0, -0.0, -0.5, -1.0, -1.5, -2.0, -3.0, -4.0, -6.0])


def pack_weight(w, fmt):
    k, n = w.shape
    w = f64(bf(w)).reshape(k // 32, 32, n)
    amax = np.abs(w).max(1)
    if fmt == "e4m3":
        byte = np.frexp(amax)[1] - 1 + 127 - 7
    else:
        mant, ex = np.frexp(amax / 6.0)
        byte = np.where(mant > 0.5, ex, ex - 1) + 127
    byte = np.clip(np.where(amax > 0, byte, 1), 1, 254)
    scaled = (w * np.exp2(127.0 - byte)[:, None, :]).reshape(k, n).astype(np.float32)
    by_word = np.ascontiguousarray(scaled.reshape(k // 512, 128, 4, n).transpose(0, 1, 3, 2))
    if fmt == "e4m3":
        words = by_word.astype(ml_dtypes.float8_e4m3fn).view(np.uint8)
    else:
        c = by_word.astype(ml_dtypes.float4_e2m1fn).view(np.uint8) & 0xF
        words = c[..., 0::2] | (c[..., 1::2] << 4)
    return np.ascontiguousarray(words), np.ascontiguousarray(byte.astype(np.uint8).reshape(k // 512, 16, n))


def unpack_weight(words, scales, fmt):
    g, p, n, _ = words.shape
    if fmt == "e4m3":
        vals = np.ascontiguousarray(words).view(ml_dtypes.float8_e4m3fn).astype(np.float64)
    else:
        nib = np.empty((g, p, n, 4), np.uint8)
        nib[..., 0::2] = words & 0xF
        nib[..., 1::2] = words >> 4
        vals = E2M1[nib]
    vals = vals * np.repeat(np.exp2(scales.astype(np.float64) - 127.0), 8, axis=1)[..., None]
    return vals.transpose(0, 1, 3, 2).reshape(g * 512, n)
def pack4(w):
    words, scales = pack_weight(w, "e2m1")
    return words.reshape(words.shape[0], 128, -1), scales


def unpack4(words, scales):
    return unpack_weight(words.reshape(words.shape[0], 128, -1, 2), scales, "e2m1")


def planes(Y):
    n, m = Y.shape
    b = f64(bf(Y)).reshape(n // 32, 32, m)
    amax = np.abs(b).max(1)
    byte = np.clip(np.where(amax > 0, np.frexp(amax)[1] - 1 + 127 - 7, 1), 1, 254)
    codes = (b * np.exp2(127.0 - byte)[:, None, :]).reshape(n, m).astype(np.float32).astype(ml_dtypes.float8_e4m3fn).view(np.uint8)
    words = codes.reshape(n // 512, 128, 4, m).transpose(0, 1, 3, 2)
    return np.ascontiguousarray(words), np.ascontiguousarray(byte.astype(np.uint8).reshape(n // 512, 16, m))


M, E, P, S, F, D = 1024, 16, 64, 1024, 1024, 2048

def setup_inputs():
    s = mx_kscale(S)
    t = mx_kscale(F)
    col = np.exp(0.8 * np.random.randn(D))
    slot_logits = bf(2.0 * np.random.randn(M, S))
    slot_scale = bf(3.0 * (1.0 + 0.1 * np.random.randn(S)) * s)
    slot_out = bf(np.random.randn(E, P, D) / s.reshape(E, P, 1))
    gate = bf(np.random.randn(M, F))
    up = bf(np.random.randn(M, F) * t)
    down_words, down_scales = pack4(1.5 * np.random.randn(F, D) / np.sqrt(F) / t[:, None])
    layer_scale = bf(col * (1.0 + 0.1 * np.random.randn(D)))
    residual = bf(0.7 * col * np.random.randn(M, D))
    return dict(slot_logits=slot_logits, slot_scale=slot_scale, slot_out=slot_out, gate=gate, up=up,
                down_words=down_words, down_scales=down_scales, layer_scale=layer_scale, residual=residual)

def reference(slot_logits, slot_scale, slot_out, gate, up, down_words, down_scales, layer_scale, residual):
    L = f64(slot_logits)
    e = np.exp(L - L.max(axis=1, keepdims=True))
    C = e / e.sum(axis=1, keepdims=True) * f64(slot_scale)
    O = f64(slot_out).reshape(S, D)
    routed = mxq(C, 1, "e4m3") @ mxq(O, 0, "e4m3")
    a = f64(gate)
    H = a / (1.0 + np.exp(-a)) * f64(up)
    shared = mxq(H, 1, "e4m3") @ unpack4(down_words, down_scales)
    y = f64(residual) + f64(layer_scale) * (routed + shared)
    Y = y.T
    words, scales = planes(Y)
    return y, words, scales

@@ -1,0 +1,457 @@
+from contextlib import ExitStack
+
+import concourse.mybir as mybir
+from concourse.masks import make_identity
+
+M, S, F, D = 1024, 1024, 1024, 2048
+FLOPS = 2 * M * S * D + 2 * M * F * D
+
+F32 = mybir.dt.float32
+BF16 = mybir.dt.bfloat16
+I32 = mybir.dt.int32
+U32 = mybir.dt.uint32
+U8 = mybir.dt.uint8
+FP8X4 = mybir.dt.float8_e4m3fn_x4
+FP4X4 = mybir.dt.float4_e2m1fn_x4
+ALU = mybir.AluOpType
+ACT = mybir.ActivationFunctionType
+
+P = 128
+PACK = 4
+K_PASS = P * PACK
+PASSES = S // K_PASS
+N_TILE = 512
+TILES = M // P
+GROUPS = D // N_TILE
+UNITS = TILES * GROUPS
+C_LAG = 3
+Y_ROUND = 3
+C_EARLY = 6
+C_OFF = 4
+GC0 = 0
+GC1 = 9
+AHEAD = 1
+O1 = (2, 4)
+G23 = 6
+G01 = 2
+GAIN1 = 9
+Y_TURN = 5
+Y_COPY = 6
+Y_QUANT = 8
+O_TICKS = [6, 8, 10, 12, 14, 16, 18, 20]
+O_LAG = 2
+LAST = 2
+
+
+def tile_slot_combine_shared_expert_g5_kernel(
+    tc, slot_logits, slot_scale, slot_out, gate, up, down_words, down_scales, layer_scale, residual,
+    out_0, out_1, out_2,
+):
+    nc = tc.nc
+    slot_rows = slot_out.rearrange("e p d -> (e p) d")
+
+    with ExitStack() as ctx:
+        keep = ctx.enter_context(tc.tile_pool(name="keep", bufs=1))
+        work = ctx.enter_context(tc.tile_pool(name="work", bufs=3))
+        psum = ctx.enter_context(tc.psum_pool(name="psum", bufs=1))
+        ctx.enter_context(tc.manual_schedule())
+
+        def bank(index, shape, dtype):
+            return psum.tile(shape, dtype, name="bank%d" % index, tag="bank%d" % index)
+
+        ident = keep.tile([P, P], F32, align_bytes=64)
+        zeros = keep.tile([P, P], BF16, align_bytes=64)
+        ones = keep.tile([P, P], BF16, align_bytes=64)
+        rows = keep.tile([P, S + D], BF16, align_bytes=64)
+        gain = keep.tile([P, D], BF16, align_bytes=64)
+        w_scales = keep.tile([P, PASSES, D], U8, align_bytes=64)
+        y_scales = keep.tile([P, M], U8, align_bytes=64)
+
+        tokens, logits, neg_max, exps, sums, inv_sum, c_sorted, c_bank, c_words = {}, {}, {}, {}, {}, {}, {}, {}, {}
+        gates, ups, g_bank, u_bank, silus, h_words = {}, {}, {}, {}, {}, {}
+        t_codes, t_scales = {}, {}
+        o_raw, o_words, o_codes, o_scales, w_words = {}, {}, {}, {}, {}
+        res, acc, y, y_sorted, y_bank, y_words, y_codes, gain_bank = {}, {}, {}, {}, {}, {}, {}, {}
+
+        def load_logits(t):
+            tokens[t] = keep.tile([P, S + F], BF16, name="tokens%d" % t, align_bytes=64)
+            logits[t] = tokens[t][:, :S]
+            nc.sync.dma_start(out=logits[t], in_=slot_logits[t * P:(t + 1) * P, :])
+
+        def load_gate_up(t):
+            gates[t] = work.tile([P, F], BF16, name="gate_rows", bufs=6, align_bytes=64)
+            ups[t] = work.tile([P, F], BF16, name="up_rows", bufs=6, align_bytes=64)
+            nc.sync.dma_start(out=gates[t][:], in_=gate[t * P:(t + 1) * P, :])
+            nc.sync.dma_start(out=ups[t][:], in_=up[t * P:(t + 1) * P, :])
+
+        def load_o(g, c):
+            o_raw[g, c] = work.tile([P, PACK, N_TILE], BF16, name="o_raw", bufs=4, align_bytes=64)
+            src = slot_rows[c * K_PASS:(c + 1) * K_PASS, g * N_TILE:(g + 1) * N_TILE]
+            nc.sync.dma_start(out=o_raw[g, c][:], in_=src.rearrange("(p j) n -> p j n", j=PACK))
+
+        def load_w():
+            for q in range(4):
+                nc.sync.dma_start(
+                    out=w_scales[32 * q:32 * q + 4, :, :].bitcast(I32),
+                    in_=down_scales[:, 4 * q:4 * q + 4, :].rearrange("c r n -> r c n").bitcast(I32),
+                )
+            for c in range(PASSES):
+                w_words[c] = keep.tile([P, 2 * D], U8, name="w_words%d" % c, align_bytes=64)
+                nc.sync.dma_start(out=w_words[c][:].bitcast(I32), in_=down_words[c].bitcast(I32))
+
+        def load_res(g, half):
+            res[g, half] = work.tile([P, 4, N_TILE], BF16, name="res_rows", bufs=3, align_bytes=64)
+            src = residual[half * 4 * P:(half + 1) * 4 * P, g * N_TILE:(g + 1) * N_TILE]
+            nc.sync.dma_start(out=res[g, half][:], in_=src.rearrange("(j p) n -> p j n", p=P))
+
+        def row_max(t):
+            neg_max[t] = work.tile([P, 1], F32, name="neg_max", bufs=TILES)
+            nc.vector.tensor_scalar(
+                out=logits[t], in0=logits[t], scalar1=-1.0, scalar2=None,
+                op0=ALU.mult, op1=ALU.min, accum_out=neg_max[t][:],
+            )
+
+        def exponentials(t):
+            exps[t] = work.tile([P, 2, 256, 2], F32, name="act_out", bufs=5, align_bytes=64)
+            sums[t] = work.tile([P, 1], F32, name="exp_sum", bufs=TILES)
+            nc.scalar.activation(
+                out=exps[t][:], in_=logits[t].rearrange("p (w u e) -> p u w e", u=2, e=2),
+                func=ACT.Exp, bias=neg_max[t][:], scale=-1.0, accum_out=sums[t][:],
+            )
+
+        def invert_sum(t):
+            inv_sum[t] = work.tile([P, 1], F32, name="inv_sum", bufs=TILES)
+            nc.vector.reciprocal(out=inv_sum[t][:], in_=sums[t][:])
+
+        def combine_weights(t):
+            c_sorted[t] = tokens[t][:, S:]
+            nc.vector.scalar_tensor_tensor(
+                out=c_sorted[t], in0=exps[t][:].rearrange("p u w e -> p (u w e)"), scalar=inv_sum[t][:],
+                in1=scale_bank[:], op0=ALU.mult, op1=ALU.mult,
+            )
+
+        def transpose_c(t):
+            c_bank[t] = bank((0, 1, 3)[t % 3] if t < C_EARLY else 3, [P, 4, P], F32)
+            words = c_sorted[t].bitcast(F32)
+            for i in range(4):
+                nc.tensor.transpose(c_bank[t][:, i, :], words[:, i * P:(i + 1) * P], ident[:])
+
+        def copy_c(t):
+            nc.scalar.copy(
+                out=tokens[t][:, :S].bitcast(F32).rearrange("p (w u) -> p w u", u=2),
+                in_=c_bank[t][:].rearrange("p (u c) m -> p (c m) u", u=2),
+            )
+
+        def quantize_tokens(t):
+            t_codes[t] = keep.tile([P, 2 * PASSES * P], U32, name="t_codes%d" % t, align_bytes=64)
+            t_scales[t] = keep.tile([P, 2 * PASSES * P], U8, name="t_scales%d" % t, align_bytes=64)
+            nc.vector.quantize_mx(out=t_codes[t][:].bitcast(FP8X4), scales=t_scales[t][:], in_=tokens[t][:])
+
+        def transpose_words(src, dst):
+            words = src[:].bitcast(F32)
+            for u in range(2):
+                for c in range(PASSES):
+                    nc.tensor.transpose(dst[:, 2 * u + c, :], words[:, 256 * c + u:256 * (c + 1):2], ident[:])
+
+        def transpose_gate(t):
+            g_bank[t] = bank(4 + t % 2, [P, 4, P], F32)
+            transpose_words(gates[t], g_bank[t])
+
+        def transpose_up(t):
+            u_bank[t] = bank((2, 6)[t % 2] if t else 7, [P, 4, P], F32)
+            transpose_words(ups[t], u_bank[t])
+
+        def word_order(tile):
+            halves = tile[:].rearrange("p i m -> p (i m)").bitcast(BF16)
+            return halves.rearrange("p (u w e) -> p w u e", u=2, e=2)
+
+        def silu(t):
+            silus[t] = work.tile([P, 2, 256, 2], F32, name="act_out", bufs=5, align_bytes=64)
+            dst = silus[t][:].rearrange("p a b c -> p (a b c)").rearrange("p (w u e) -> p w u e", u=2, e=2)
+            nc.scalar.activation(out=dst, in_=word_order(g_bank[t]), func=ACT.Silu)
+
+        def gate_up_product(t):
+            act = silus[t][:].rearrange("p a b c -> p (a b c)").rearrange("p (w u e) -> p w u e", u=2, e=2)
+            nc.vector.tensor_tensor(
+                out=tokens[t][:, S:].rearrange("p (w u e) -> p w u e", u=2, e=2),
+                in0=word_order(u_bank[t]), in1=act, op=ALU.mult,
+            )
+
+        def interleave_o(g, piece, copy):
+            c, half = divmod(piece, 2)
+            if half == 0:
+                o_words[g, c] = work.tile([P, N_TILE, PACK], BF16, name="o_words", bufs=4, align_bytes=64)
+            cols = slice(half * 256, (half + 1) * 256)
+            copy(
+                out=o_words[g, c][:, cols, :].rearrange("p (n i) t -> p n t i", i=4),
+                in_=o_raw[g, c][:, :, cols].rearrange("p t (n i) -> p n t i", i=4),
+            )
+
+        def interleave_o_early(g, c):
+            o_words[g, c] = work.tile([P, N_TILE, PACK], BF16, name="o_words", bufs=4, align_bytes=64)
+            nc.gpsimd.tensor_scalar(
+                out=o_words[g, c][:], in0=o_raw[g, c][:].rearrange("p t n -> p n t"),
+                scalar1=1.0, scalar2=0.0, op0=ALU.mult, op1=ALU.add,
+            )
+
+        def quantize_o(g, c):
+            o_codes[g, c] = work.tile([P, N_TILE], U32, name="o_codes", bufs=6, align_bytes=64)
+            o_scales[g, c] = work.tile([P, N_TILE], U8, name="o_scales", bufs=6, align_bytes=64)
+            nc.vector.quantize_mx(
+                out=o_codes[g, c][:].bitcast(FP8X4), scales=o_scales[g, c][:],
+                in_=o_words[g, c][:].rearrange("p n t -> p (n t)"),
+            )
+
+        batches = []
+        for g in range(GROUPS):
+            for t in range(0, TILES, 2):
+                if g == GROUPS - 1 and t == TILES - 2:
+                    batches.append((g, t, 1))
+                    batches.append((g, t + 1, 1))
+                else:
+                    batches.append((g, t, 2))
+        batch_of = {}
+        for b, (g, t0, count) in enumerate(batches):
+            for t in range(t0, t0 + count):
+                batch_of[g * TILES + t] = b
+
+        def multiply(unit):
+            g, t = divmod(unit, TILES)
+            acc[unit] = bank((0, 1, 7)[unit % 3] if unit < TILES else (4, 5, 0, 1, 7, 6)[(unit - TILES) % 6], [P, N_TILE], F32)
+            cols = slice(g * N_TILE, (g + 1) * N_TILE)
+            for c in range(PASSES):
+                tok = slice(c * P, (c + 1) * P)
+                nc.tensor.matmul_mx(
+                    out=acc[unit][:], lhsT=t_codes[t][:, tok].bitcast(FP8X4), lhsT_scale=t_scales[t][:, tok],
+                    rhs=o_codes[g, c][:].bitcast(FP8X4), rhs_scale=o_scales[g, c][:],
+                    start=(c == 0), stop=False,
+                )
+            for c in range(PASSES):
+                tok = slice((PASSES + c) * P, (PASSES + c + 1) * P)
+                nc.tensor.matmul_mx(
+                    out=acc[unit][:], lhsT=t_codes[t][:, tok].bitcast(FP8X4), lhsT_scale=t_scales[t][:, tok],
+                    rhs=w_words[c][:, 2 * g * N_TILE:2 * (g + 1) * N_TILE].bitcast(FP4X4),
+                    rhs_scale=w_scales[:, c, cols],
+                    start=False, stop=(c == PASSES - 1),
+                )
+
+        def apply_gain(unit):
+            g, t = divmod(unit, TILES)
+            b = batch_of[unit]
+            t0 = batches[b][1]
+            if t == t0:
+                y[b] = work.tile([P, 2 * N_TILE], F32, name="y_rows", bufs=4, align_bytes=64)
+            nc.vector.tensor_tensor(
+                out=y[b][:, (t - t0) * N_TILE:(t - t0 + 1) * N_TILE], in0=acc[unit][:],
+                in1=gain[:, g * N_TILE:(g + 1) * N_TILE], op=ALU.mult,
+            )
+
+        def add_residual(b):
+            g, t0, count = batches[b]
+            half, j = divmod(t0, 4)
+            rows_y = y[b][:, :count * N_TILE]
+            nc.vector.tensor_tensor(
+                out=rows_y, in0=rows_y,
+                in1=res[g, half][:, j:j + count, :].rearrange("p j n -> p (j n)"), op=ALU.add,
+            )
+            dst = out_0[t0 * P:(t0 + count) * P, g * N_TILE:(g + 1) * N_TILE]
+            nc.sync.dma_start(
+                out=dst.rearrange("(j p) n -> p j n", p=P),
+                in_=rows_y.rearrange("p (j n) -> p j n", n=N_TILE),
+            )
+
+        def round_y(b, copy):
+            count = batches[b][2]
+            y_sorted[b] = work.tile([P, 2 * N_TILE], BF16, name="y_sorted", bufs=4, align_bytes=64)
+            copy(
+                out=y_sorted[b][:, :count * N_TILE].rearrange("p (u w e) -> p u w e", u=2, e=2),
+                in_=y[b][:, :count * N_TILE].rearrange("p (w u e) -> p u w e", u=2, e=2),
+            )
+
+        def transpose_y(b):
+            count = batches[b][2]
+            y_bank[b] = bank(3 if b < 3 else 2 + b % 2, [P, 4, P], F32)
+            words = y_sorted[b][:].bitcast(F32)
+            for i in range(2 * count):
+                nc.tensor.transpose(y_bank[b][:, i, :], words[:, i * P:(i + 1) * P], ident[:])
+
+        def copy_y(b, copy):
+            count = batches[b][2]
+            y_words[b] = work.tile([P, 2 * N_TILE], BF16, name="y_words", bufs=3, align_bytes=64)
+            copy(
+                out=y_words[b][:, :count * N_TILE].bitcast(F32).rearrange("p (w u) -> p w u", u=2),
+                in_=y_bank[b][:, :2 * count, :].rearrange("p (u j) m -> p (j m) u", u=2),
+            )
+
+        def quantize_y(b):
+            g, t0, count = batches[b]
+            if t0 == 0:
+                y_codes[g] = work.tile([P, M], U32, name="y_codes", bufs=2, align_bytes=64)
+            tok = slice(t0 * P, (t0 + count) * P)
+            nc.vector.quantize_mx(
+                out=y_codes[g][:, tok].bitcast(FP8X4), scales=y_scales[4 * g:P, tok],
+                in_=y_words[b][:, :count * N_TILE],
+            )
+            done = t0 + count
+            first = {4: 0, 8: 4} if g < GROUPS - 1 else {4: 0, 7: 4, 8: 7}
+            if done in first:
+                tok = slice(first[done] * P, done * P)
+                dst = out_1[g].rearrange("p m t -> p (m t)").bitcast(I32)
+                nc.sync.dma_start(out=dst[:, tok], in_=y_codes[g][:, tok].bitcast(I32))
+
+        def spread_gain(half):
+            gain_bank[half] = bank(3 - half, [P, 2 * N_TILE], BF16)
+            for i in range(2):
+                col = S + (2 * half + i) * N_TILE
+                nc.tensor.matmul(
+                    gain_bank[half][:, i * N_TILE:(i + 1) * N_TILE], lhsT=ones[:], rhs=rows[:, col:col + N_TILE],
+                    start=True, stop=True,
+                )
+
+        def copy_gain(half):
+            nc.scalar.copy(out=gain[:, half * 2 * N_TILE:(half + 1) * 2 * N_TILE], in_=gain_bank[half][:])
+
+        nc.vector.memset(zeros[:].bitcast(I32), 0)
+        nc.vector.memset(rows[:].bitcast(I32), 0)
+        nc.scalar.activation(out=ones[:], in_=zeros[:], func=ACT.Exp)
+        make_identity(nc, ident[:])
+        nc.gpsimd.memset(w_scales[:].rearrange("p c n -> p (c n)").bitcast(I32), 0)
+
+        load_logits(0)
+        load_logits(1)
+        nc.sync.dma_start(out=rows[0:1, :S], in_=slot_scale.rearrange("(o s) -> o s", o=1))
+        nc.sync.dma_start(out=rows[0:1, S:], in_=layer_scale.rearrange("(o d) -> o d", o=1))
+        for t in range(2, TILES):
+            load_logits(t)
+        load_o(0, 0)
+        load_o(0, 1)
+        load_gate_up(0)
+        load_o(1, 0)
+        load_gate_up(1)
+        load_o(1, 1)
+        load_gate_up(2)
+        load_w()
+        load_gate_up(3)
+        load_res(0, 0)
+        load_gate_up(4)
+        load_gate_up(5)
+        for g in range(2):
+            for c in range(PASSES):
+                interleave_o_early(g, c)
+        load_o(2, 0)
+        load_res(0, 1)
+        load_o(2, 1)
+        load_res(1, 0)
+        load_o(3, 0)
+        load_o(3, 1)
+
+        scale_bank = bank(2, [P, S], BF16)
+        sorted_scale = rows[:, :S].rearrange("p (w u e) -> p u w e", u=2, e=2)
+        for u in range(2):
+            nc.tensor.matmul(
+                scale_bank[:, u * N_TILE:(u + 1) * N_TILE], lhsT=ones[:], rhs=sorted_scale[:, u, :, :],
+                start=True, stop=True,
+            )
+
+        spread_gain(0)
+
+        for t in range(TILES):
+            row_max(t)
+            if t < 4:
+                exponentials(t)
+            if t >= TILES - 2:
+                invert_sum(t - (TILES - 2))
+
+        last_unit_of = {g * TILES + t0 + count - 1: b for b, (g, t0, count) in enumerate(batches)}
+        o_ticks = O_TICKS
+        for step in range(TILES + UNITS + 2):
+            tick = step - TILES
+            if tick == GAIN1:
+                spread_gain(1)
+            if 0 <= tick - 1 < TILES:
+                multiply(tick - 1)
+            if TILES <= tick + AHEAD < UNITS:
+                multiply(tick + AHEAD)
+            if tick - Y_TURN in last_unit_of:
+                transpose_y(last_unit_of[tick - Y_TURN])
+            if step - G01 in (0, 1):
+                transpose_gate(step - G01)
+                transpose_up(step - G01)
+            if step == G23:
+                transpose_gate(2)
+            if 3 <= tick + 2 < TILES:
+                transpose_gate(tick + 2)
+            if C_EARLY <= tick + C_OFF < TILES and tick >= 1:
+                transpose_c(tick + C_OFF)
+            if step + 4 < TILES:
+                exponentials(step + 4)
+            if step in (4, 5):
+                silu(step - 4)
+            if 2 <= tick + 2 < TILES:
+                silu(tick + 2)
+            if 0 <= step - 2 < C_EARLY:
+                copy_c(step - 2)
+            if C_EARLY <= tick + C_OFF < TILES and tick >= 1:
+                copy_c(tick + C_OFF)
+            if step == GC0:
+                copy_gain(0)
+            if tick == GC1:
+                copy_gain(1)
+            if tick in o_ticks:
+                interleave_o(2 + o_ticks.index(tick) // 4, o_ticks.index(tick) % 4, nc.scalar.copy)
+            if tick - Y_ROUND in last_unit_of:
+                round_y(last_unit_of[tick - Y_ROUND], nc.scalar.copy)
+            if tick - Y_COPY in last_unit_of:
+                copy_y(last_unit_of[tick - Y_COPY], nc.scalar.copy)
+            if step < TILES:
+                combine_weights(step)
+                if step < C_EARLY:
+                    transpose_c(step)
+                if step + 2 < TILES:
+                    invert_sum(step + 2)
+            if 0 <= tick < TILES:
+                gate_up_product(tick)
+            if 2 <= tick + 2 < TILES:
+                transpose_up(tick + 2)
+            if tick in (0, 1):
+                load_gate_up(tick + 6)
+            if 0 <= tick - 2 < UNITS:
+                apply_gain(tick - 2)
+            if tick == 0:
+                quantize_o(0, 0)
+            if 0 <= tick < TILES:
+                quantize_tokens(tick)
+            if tick == 0:
+                quantize_o(0, 1)
+            if tick in O1:
+                quantize_o(1, O1.index(tick))
+            if tick - O_LAG in o_ticks[1::2]:
+                g, c = divmod(2 * PASSES + o_ticks[1::2].index(tick - O_LAG), PASSES)
+                quantize_o(g, c)
+            if tick - Y_QUANT in last_unit_of:
+                quantize_y(last_unit_of[tick - Y_QUANT])
+            if tick - 2 in last_unit_of:
+                add_residual(last_unit_of[tick - 2])
+                g, t0, count = batches[last_unit_of[tick - 2]]
+                nxt = 2 * g + (t0 + count) // 4 + 2
+                if (t0 + count) % 4 == 0 and nxt < 2 * GROUPS:
+                    load_res(nxt // 2, nxt % 2)
+
+        last = len(batches) - 1
+        transpose_y(last - 2)
+        copy_y(last - 2, nc.scalar.copy)
+        transpose_y(last - 1)
+        quantize_y(last - 3)
+        round_y(last, nc.vector.tensor_copy)
+        copy_y(last - 1, nc.scalar.copy)
+        transpose_y(last)
+        quantize_y(last - 2)
+        quantize_y(last - 1)
+        copy_y(last, nc.vector.tensor_copy)
+        quantize_y(last)
+
+        for q in range(4):
+            nc.sync.dma_start(
+                out=out_2[:, 4 * q:4 * q + 4, :].bitcast(I32),
+                in_=y_scales[32 * q:32 * q + 16, :].bitcast(I32),
+            )

@@ -24,23 +24,20 @@ N_TILE = 512
 TILES = M // P
 GROUPS = D // N_TILE
 UNITS = TILES * GROUPS
-C_LAG = 3
-Y_ROUND = 3
-C_EARLY = 6
-C_OFF = 4
-GC0 = 0
-GC1 = 9
-AHEAD = 1
-O1 = (2, 4)
-G23 = 6
-G01 = 2
-GAIN1 = 9
-Y_TURN = 5
-Y_COPY = 6
-Y_QUANT = 8
-O_TICKS = [6, 8, 10, 12, 14, 16, 18, 20]
-O_LAG = 2
-LAST = 2
+HALF = TILES // 2
+ACC_BANKS = 6
+POOL = 512
+PA = (0, 2, 4, 6, 8, 8, 8, 8)
+RL = 1
+QL = 2
+EARLY = 4
+G1 = 2
+SL = 2
+H6 = 1
+YB = 3
+TA = 1
+QA = (0, 0, 1, 2, 3, 4, 4, 4)
+L_FIRST = 6
 
 
 def tile_slot_combine_shared_expert_g5_kernel(
@@ -69,7 +66,7 @@ def tile_slot_combine_shared_expert_g5_kernel(
 
         tokens, logits, neg_max, exps, sums, inv_sum, c_sorted, c_bank, c_words = {}, {}, {}, {}, {}, {}, {}, {}, {}
         gates, ups, g_bank, u_bank, silus, h_words = {}, {}, {}, {}, {}, {}
-        t_codes, t_scales = {}, {}
+        t_codes, t_scales, t_bank = {}, {}, {}
         o_raw, o_words, o_codes, o_scales, w_words = {}, {}, {}, {}, {}
         res, acc, y, y_sorted, y_bank, y_words, y_codes, gain_bank = {}, {}, {}, {}, {}, {}, {}, {}
 
@@ -79,9 +76,9 @@ def tile_slot_combine_shared_expert_g5_kernel(
             nc.sync.dma_start(out=logits[t], in_=slot_logits[t * P:(t + 1) * P, :])
 
         def load_gate_up(t):
-            gates[t] = work.tile([P, F], BF16, name="gate_rows", bufs=6, align_bytes=64)
-            ups[t] = work.tile([P, F], BF16, name="up_rows", bufs=6, align_bytes=64)
-            nc.sync.dma_start(out=gates[t][:], in_=gate[t * P:(t + 1) * P, :])
+            gates[t] = tokens[t][:, S:]
+            ups[t] = work.tile([P, F], BF16, name="up_rows", bufs=TILES, align_bytes=64)
+            nc.sync.dma_start(out=gates[t], in_=gate[t * P:(t + 1) * P, :])
             nc.sync.dma_start(out=ups[t][:], in_=up[t * P:(t + 1) * P, :])
 
         def load_o(g, c):
@@ -124,22 +121,22 @@ def tile_slot_combine_shared_expert_g5_kernel(
             nc.vector.reciprocal(out=inv_sum[t][:], in_=sums[t][:])
 
         def combine_weights(t):
-            c_sorted[t] = tokens[t][:, S:]
             nc.vector.scalar_tensor_tensor(
-                out=c_sorted[t], in0=exps[t][:].rearrange("p u w e -> p (u w e)"), scalar=inv_sum[t][:],
+                out=tokens[t][:, :S], in0=exps[t][:].rearrange("p u w e -> p (u w e)"), scalar=inv_sum[t][:],
                 in1=scale_bank[:], op0=ALU.mult, op1=ALU.mult,
             )
 
-        def transpose_c(t):
-            c_bank[t] = bank((0, 1, 3)[t % 3] if t < C_EARLY else 3, [P, 4, P], F32)
-            words = c_sorted[t].bitcast(F32)
+        def transpose_tokens(t, part, index):
+            words = tokens[t][:].bitcast(F32)
+            t_bank[t, part] = bank(index, [P, 4, P], F32)
             for i in range(4):
-                nc.tensor.transpose(c_bank[t][:, i, :], words[:, i * P:(i + 1) * P], ident[:])
+                col = (4 * part + i) * P
+                nc.tensor.transpose(t_bank[t, part][:, i, :], words[:, col:col + P], ident[:])
 
-        def copy_c(t):
+        def copy_tokens(t, part):
             nc.scalar.copy(
-                out=tokens[t][:, :S].bitcast(F32).rearrange("p (w u) -> p w u", u=2),
-                in_=c_bank[t][:].rearrange("p (u c) m -> p (c m) u", u=2),
+                out=tokens[t][:, part * S:(part + 1) * S].bitcast(F32).rearrange("p (w u) -> p w u", u=2),
+                in_=t_bank[t, part][:].rearrange("p (u c) m -> p (c m) u", u=2),
             )
 
         def quantize_tokens(t):
@@ -147,34 +144,16 @@ def tile_slot_combine_shared_expert_g5_kernel(
             t_scales[t] = keep.tile([P, 2 * PASSES * P], U8, name="t_scales%d" % t, align_bytes=64)
             nc.vector.quantize_mx(out=t_codes[t][:].bitcast(FP8X4), scales=t_scales[t][:], in_=tokens[t][:])
 
-        def transpose_words(src, dst):
-            words = src[:].bitcast(F32)
-            for u in range(2):
-                for c in range(PASSES):
-                    nc.tensor.transpose(dst[:, 2 * u + c, :], words[:, 256 * c + u:256 * (c + 1):2], ident[:])
-
-        def transpose_gate(t):
-            g_bank[t] = bank(4 + t % 2, [P, 4, P], F32)
-            transpose_words(gates[t], g_bank[t])
-
-        def transpose_up(t):
-            u_bank[t] = bank((2, 6)[t % 2] if t else 7, [P, 4, P], F32)
-            transpose_words(ups[t], u_bank[t])
-
-        def word_order(tile):
-            halves = tile[:].rearrange("p i m -> p (i m)").bitcast(BF16)
-            return halves.rearrange("p (u w e) -> p w u e", u=2, e=2)
-
         def silu(t):
             silus[t] = work.tile([P, 2, 256, 2], F32, name="act_out", bufs=5, align_bytes=64)
-            dst = silus[t][:].rearrange("p a b c -> p (a b c)").rearrange("p (w u e) -> p w u e", u=2, e=2)
-            nc.scalar.activation(out=dst, in_=word_order(g_bank[t]), func=ACT.Silu)
+            nc.scalar.activation(
+                out=silus[t][:], in_=gates[t].rearrange("p (w u e) -> p u w e", u=2, e=2), func=ACT.Silu,
+            )
 
         def gate_up_product(t):
-            act = silus[t][:].rearrange("p a b c -> p (a b c)").rearrange("p (w u e) -> p w u e", u=2, e=2)
             nc.vector.tensor_tensor(
-                out=tokens[t][:, S:].rearrange("p (w u e) -> p w u e", u=2, e=2),
-                in0=word_order(u_bank[t]), in1=act, op=ALU.mult,
+                out=tokens[t][:, S:].rearrange("p (u w e) -> p u w e", u=2, e=2),
+                in0=silus[t][:], in1=ups[t][:].rearrange("p (w u e) -> p u w e", u=2, e=2), op=ALU.mult,
             )
 
         def interleave_o(g, piece, copy):
@@ -202,105 +181,99 @@ def tile_slot_combine_shared_expert_g5_kernel(
                 in_=o_words[g, c][:].rearrange("p n t -> p (n t)"),
             )
 
-        batches = []
-        for g in range(GROUPS):
-            for t in range(0, TILES, 2):
-                if g == GROUPS - 1 and t == TILES - 2:
-                    batches.append((g, t, 1))
-                    batches.append((g, t + 1, 1))
-                else:
-                    batches.append((g, t, 2))
-        batch_of = {}
-        for b, (g, t0, count) in enumerate(batches):
-            for t in range(t0, t0 + count):
-                batch_of[g * TILES + t] = b
+        batches = [(0, 0, 4), (1, 0, 4), (0, 4, 4), (1, 4, 4), (2, 0, 4), (2, 4, 4), (3, 0, 4), (3, 4, 2), (3, 6, 2)]
+        units = [(b, j) for b, batch in enumerate(batches) for j in range(batch[2])]
 
         def multiply(unit):
-            g, t = divmod(unit, TILES)
-            acc[unit] = bank((0, 1, 7)[unit % 3] if unit < TILES else (4, 5, 0, 1, 7, 6)[(unit - TILES) % 6], [P, N_TILE], F32)
+            b, j = units[unit]
+            g, t = batches[b][0], batches[b][1] + j
+            acc[unit] = bank(unit % ACC_BANKS, [P, N_TILE], F32)
             cols = slice(g * N_TILE, (g + 1) * N_TILE)
+            passes = []
             for c in range(PASSES):
+                passes.append((c, o_codes[g, c][:].bitcast(FP8X4), o_scales[g, c][:]))
+            for c in range(PASSES):
+                words = w_words[c][:, 2 * g * N_TILE:2 * (g + 1) * N_TILE]
+                passes.append((PASSES + c, words.bitcast(FP4X4), w_scales[:, c, cols]))
+            for i, (c, rhs, rhs_scale) in enumerate(passes[:1] + passes[2:] + passes[1:2]):
                 tok = slice(c * P, (c + 1) * P)
                 nc.tensor.matmul_mx(
                     out=acc[unit][:], lhsT=t_codes[t][:, tok].bitcast(FP8X4), lhsT_scale=t_scales[t][:, tok],
-                    rhs=o_codes[g, c][:].bitcast(FP8X4), rhs_scale=o_scales[g, c][:],
-                    start=(c == 0), stop=False,
-                )
-            for c in range(PASSES):
-                tok = slice((PASSES + c) * P, (PASSES + c + 1) * P)
-                nc.tensor.matmul_mx(
-                    out=acc[unit][:], lhsT=t_codes[t][:, tok].bitcast(FP8X4), lhsT_scale=t_scales[t][:, tok],
-                    rhs=w_words[c][:, 2 * g * N_TILE:2 * (g + 1) * N_TILE].bitcast(FP4X4),
-                    rhs_scale=w_scales[:, c, cols],
-                    start=False, stop=(c == PASSES - 1),
+                    rhs=rhs, rhs_scale=rhs_scale, start=(i == 0), stop=(i == len(passes) - 1),
                 )
 
         def apply_gain(unit):
-            g, t = divmod(unit, TILES)
-            b = batch_of[unit]
-            t0 = batches[b][1]
-            if t == t0:
-                y[b] = work.tile([P, 2 * N_TILE], F32, name="y_rows", bufs=4, align_bytes=64)
+            b, j = units[unit]
+            g = batches[b][0]
+            if j == 0:
+                y[b] = work.tile([P, 4 * N_TILE], F32, name="y_rows", bufs=YB, align_bytes=64)
             nc.vector.tensor_tensor(
-                out=y[b][:, (t - t0) * N_TILE:(t - t0 + 1) * N_TILE], in0=acc[unit][:],
+                out=y[b][:, j * N_TILE:(j + 1) * N_TILE], in0=acc[unit][:],
                 in1=gain[:, g * N_TILE:(g + 1) * N_TILE], op=ALU.mult,
             )
 
-        def add_residual(b):
+        def add_residual(engine, b, first, end):
             g, t0, count = batches[b]
             half, j = divmod(t0, 4)
-            rows_y = y[b][:, :count * N_TILE]
-            nc.vector.tensor_tensor(
-                out=rows_y, in0=rows_y,
-                in1=res[g, half][:, j:j + count, :].rearrange("p j n -> p (j n)"), op=ALU.add,
+            rows_r = res[g, half][:].rearrange("p j n -> p (j n)")
+            engine.tensor_tensor(
+                out=y[b][:, first:end], in0=y[b][:, first:end],
+                in1=rows_r[:, j * N_TILE + first:j * N_TILE + end], op=ALU.add,
             )
+
+        def store_y(b):
+            g, t0, count = batches[b]
             dst = out_0[t0 * P:(t0 + count) * P, g * N_TILE:(g + 1) * N_TILE]
             nc.sync.dma_start(
                 out=dst.rearrange("(j p) n -> p j n", p=P),
-                in_=rows_y.rearrange("p (j n) -> p j n", n=N_TILE),
+                in_=y[b][:, :count * N_TILE].rearrange("p (j n) -> p j n", n=N_TILE),
             )
 
-        def round_y(b, copy):
+        def round_y(b, copy, first=0, end=None):
             count = batches[b][2]
-            y_sorted[b] = work.tile([P, 2 * N_TILE], BF16, name="y_sorted", bufs=4, align_bytes=64)
+            if first == 0:
+                y_sorted[b] = work.tile([P, 4 * N_TILE], BF16, name="y_sorted", bufs=3, align_bytes=64)
+            part = slice(first * P, (end or count) * P)
             copy(
-                out=y_sorted[b][:, :count * N_TILE].rearrange("p (u w e) -> p u w e", u=2, e=2),
-                in_=y[b][:, :count * N_TILE].rearrange("p (w u e) -> p u w e", u=2, e=2),
+                out=y_sorted[b][:, :count * N_TILE].rearrange("p (u w e) -> p u w e", u=2, e=2)[:, :, part, :],
+                in_=y[b][:, :count * N_TILE].rearrange("p (w u e) -> p u w e", u=2, e=2)[:, :, part, :],
             )
 
         def transpose_y(b):
             count = batches[b][2]
-            y_bank[b] = bank(3 if b < 3 else 2 + b % 2, [P, 4, P], F32)
             words = y_sorted[b][:].bitcast(F32)
-            for i in range(2 * count):
-                nc.tensor.transpose(y_bank[b][:, i, :], words[:, i * P:(i + 1) * P], ident[:])
+            for part in range((count + 1) // 2):
+                width = min(2, count)
+                y_bank[b, part] = bank(6 + part if count == 4 else b % 2, [P, 4, P], F32)
+                for u in range(2):
+                    for j in range(width):
+                        col = (u * count + 2 * part + j) * P
+                        nc.tensor.transpose(y_bank[b, part][:, u * width + j, :], words[:, col:col + P], ident[:])
 
         def copy_y(b, copy):
             count = batches[b][2]
-            y_words[b] = work.tile([P, 2 * N_TILE], BF16, name="y_words", bufs=3, align_bytes=64)
-            copy(
-                out=y_words[b][:, :count * N_TILE].bitcast(F32).rearrange("p (w u) -> p w u", u=2),
-                in_=y_bank[b][:, :2 * count, :].rearrange("p (u j) m -> p (j m) u", u=2),
-            )
+            width = min(2, count)
+            y_words[b] = work.tile([P, 4 * N_TILE], BF16, name="y_words", bufs=4, align_bytes=64)
+            for part in range((count + 1) // 2):
+                dst = y_words[b][:, 2 * part * N_TILE:(2 * part + width) * N_TILE]
+                copy(
+                    out=dst.bitcast(F32).rearrange("p (w u) -> p w u", u=2),
+                    in_=y_bank[b, part][:, :2 * width, :].rearrange("p (u j) m -> p (j m) u", u=2),
+                )
 
         def quantize_y(b):
             g, t0, count = batches[b]
-            if t0 == 0:
-                y_codes[g] = work.tile([P, M], U32, name="y_codes", bufs=2, align_bytes=64)
+            y_codes[b] = work.tile([P, 4 * P], U32, name="y_codes", bufs=4, align_bytes=64)
             tok = slice(t0 * P, (t0 + count) * P)
             nc.vector.quantize_mx(
-                out=y_codes[g][:, tok].bitcast(FP8X4), scales=y_scales[4 * g:P, tok],
+                out=y_codes[b][:, :count * P].bitcast(FP8X4), scales=y_scales[4 * g:P, tok],
                 in_=y_words[b][:, :count * N_TILE],
             )
-            done = t0 + count
-            first = {4: 0, 8: 4} if g < GROUPS - 1 else {4: 0, 7: 4, 8: 7}
-            if done in first:
-                tok = slice(first[done] * P, done * P)
-                dst = out_1[g].rearrange("p m t -> p (m t)").bitcast(I32)
-                nc.sync.dma_start(out=dst[:, tok], in_=y_codes[g][:, tok].bitcast(I32))
+            dst = out_1[g].rearrange("p m t -> p (m t)").bitcast(I32)
+            nc.sync.dma_start(out=dst[:, tok], in_=y_codes[b][:, :count * P].bitcast(I32))
 
         def spread_gain(half):
-            gain_bank[half] = bank(3 - half, [P, 2 * N_TILE], BF16)
+            gain_bank[half] = bank(6 - half, [P, 2 * N_TILE], BF16)
             for i in range(2):
                 col = S + (2 * half + i) * N_TILE
                 nc.tensor.matmul(
@@ -321,31 +294,33 @@ def tile_slot_combine_shared_expert_g5_kernel(
         load_logits(1)
         nc.sync.dma_start(out=rows[0:1, :S], in_=slot_scale.rearrange("(o s) -> o s", o=1))
         nc.sync.dma_start(out=rows[0:1, S:], in_=layer_scale.rearrange("(o d) -> o d", o=1))
-        for t in range(2, TILES):
+        for t in range(2, L_FIRST):
             load_logits(t)
         load_o(0, 0)
+        for t in range(L_FIRST, TILES):
+            load_logits(t)
         load_o(0, 1)
-        load_gate_up(0)
         load_o(1, 0)
-        load_gate_up(1)
+        load_gate_up(0)
         load_o(1, 1)
+        load_gate_up(1)
         load_gate_up(2)
-        load_w()
         load_gate_up(3)
+        load_w()
+        for t in range(4, TILES):
+            load_gate_up(t)
         load_res(0, 0)
-        load_gate_up(4)
-        load_gate_up(5)
         for g in range(2):
             for c in range(PASSES):
                 interleave_o_early(g, c)
         load_o(2, 0)
-        load_res(0, 1)
-        load_o(2, 1)
         load_res(1, 0)
+        load_o(2, 1)
+        load_res(0, 1)
         load_o(3, 0)
         load_o(3, 1)
 
-        scale_bank = bank(2, [P, S], BF16)
+        scale_bank = bank(7, [P, S], BF16)
         sorted_scale = rows[:, :S].rearrange("p (w u e) -> p u w e", u=2, e=2)
         for u in range(2):
             nc.tensor.matmul(
@@ -355,103 +330,148 @@ def tile_slot_combine_shared_expert_g5_kernel(
 
         spread_gain(0)
 
-        for t in range(TILES):
+        for t in range(L_FIRST):
             row_max(t)
             if t < 4:
                 exponentials(t)
-            if t >= TILES - 2:
-                invert_sum(t - (TILES - 2))
-
-        last_unit_of = {g * TILES + t0 + count - 1: b for b, (g, t0, count) in enumerate(batches)}
-        o_ticks = O_TICKS
-        for step in range(TILES + UNITS + 2):
-            tick = step - TILES
-            if tick == GAIN1:
-                spread_gain(1)
-            if 0 <= tick - 1 < TILES:
-                multiply(tick - 1)
-            if TILES <= tick + AHEAD < UNITS:
-                multiply(tick + AHEAD)
-            if tick - Y_TURN in last_unit_of:
-                transpose_y(last_unit_of[tick - Y_TURN])
-            if step - G01 in (0, 1):
-                transpose_gate(step - G01)
-                transpose_up(step - G01)
-            if step == G23:
-                transpose_gate(2)
-            if 3 <= tick + 2 < TILES:
-                transpose_gate(tick + 2)
-            if C_EARLY <= tick + C_OFF < TILES and tick >= 1:
-                transpose_c(tick + C_OFF)
-            if step + 4 < TILES:
-                exponentials(step + 4)
-            if step in (4, 5):
-                silu(step - 4)
-            if 2 <= tick + 2 < TILES:
-                silu(tick + 2)
-            if 0 <= step - 2 < C_EARLY:
-                copy_c(step - 2)
-            if C_EARLY <= tick + C_OFF < TILES and tick >= 1:
-                copy_c(tick + C_OFF)
-            if step == GC0:
+            if t >= L_FIRST - 2:
+                invert_sum(t - (L_FIRST - 2))
+        for t in range(TILES):
+            if t == 0:
                 copy_gain(0)
-            if tick == GC1:
+            if t + 4 < TILES and t + 4 < L_FIRST + t:
+                exponentials(t + 4)
+            if t in (4, 5):
+                silu(t - 4)
+            if t == 6:
+                copy_tokens(0, 0)
+                silu(2)
+                copy_tokens(1, 0)
+            combine_weights(t)
+            if t < EARLY:
+                transpose_tokens(t, 0, t)
+            if t + L_FIRST < TILES:
+                row_max(t + L_FIRST)
+            if t + 2 < TILES:
+                invert_sum(t + 2)
+
+        def hidden(t):
+            gate_up_product(t)
+            if 1 <= t and t + SL < TILES and t + SL > 3:
+                silu(t + SL)
+            if t < EARLY:
+                transpose_tokens(t, 1, 6 + t % 2)
+                if t >= 2:
+                    copy_tokens(t, 0)
+            else:
+                transpose_tokens(t, 0, 6)
+                transpose_tokens(t, 1, 7)
+                copy_tokens(t, 0)
+            copy_tokens(t, 1)
+            if t == 0:
+                silu(3)
+                spread_gain(1)
+            if t == G1:
                 copy_gain(1)
-            if tick in o_ticks:
-                interleave_o(2 + o_ticks.index(tick) // 4, o_ticks.index(tick) % 4, nc.scalar.copy)
-            if tick - Y_ROUND in last_unit_of:
-                round_y(last_unit_of[tick - Y_ROUND], nc.scalar.copy)
-            if tick - Y_COPY in last_unit_of:
-                copy_y(last_unit_of[tick - Y_COPY], nc.scalar.copy)
-            if step < TILES:
-                combine_weights(step)
-                if step < C_EARLY:
-                    transpose_c(step)
-                if step + 2 < TILES:
-                    invert_sum(step + 2)
-            if 0 <= tick < TILES:
-                gate_up_product(tick)
-            if 2 <= tick + 2 < TILES:
-                transpose_up(tick + 2)
-            if tick in (0, 1):
-                load_gate_up(tick + 6)
-            if 0 <= tick - 2 < UNITS:
-                apply_gain(tick - 2)
-            if tick == 0:
-                quantize_o(0, 0)
-            if 0 <= tick < TILES:
-                quantize_tokens(tick)
-            if tick == 0:
-                quantize_o(0, 1)
-            if tick in O1:
-                quantize_o(1, O1.index(tick))
-            if tick - O_LAG in o_ticks[1::2]:
-                g, c = divmod(2 * PASSES + o_ticks[1::2].index(tick - O_LAG), PASSES)
-                quantize_o(g, c)
-            if tick - Y_QUANT in last_unit_of:
-                quantize_y(last_unit_of[tick - Y_QUANT])
-            if tick - 2 in last_unit_of:
-                add_residual(last_unit_of[tick - 2])
-                g, t0, count = batches[last_unit_of[tick - 2]]
-                nxt = 2 * g + (t0 + count) // 4 + 2
-                if (t0 + count) % 4 == 0 and nxt < 2 * GROUPS:
-                    load_res(nxt // 2, nxt % 2)
+
+        hidden(0)
+        quantize_o(0, 0)
+        hidden(1)
+        quantize_tokens(0)
+        quantize_o(0, 1)
+        multiply(0)
+        hidden(2)
+        quantize_o(1, 0)
+        quantize_tokens(1)
+        multiply(1)
+        hidden(3)
+        quantize_o(1, 1)
+        multiply(4)
+        quantize_tokens(2)
+        multiply(2)
+        hidden(4)
+        quantize_tokens(3)
+        multiply(3)
+        hidden(5)
+        multiply(5)
+        if H6:
+            hidden(6)
+        quantize_tokens(4)
+
+        def advance(limit):
+            for later in range(len(acc), min(limit + 1, UNITS)):
+                g, t0, count = batches[units[later][0]]
+                if later == len(acc) and t0 + units[later][1] in t_codes and (g, 1) in o_codes:
+                    multiply(later)
+
+        pieces = [(g, piece) for g in (2, 3) for piece in range(4)]
+        unit = 0
+        for b in range(len(batches) - 2):
+            if b >= 2:
+                round_y(b - RL, nc.scalar.copy)
+            for g, piece in pieces[PA[b]:PA[b + 1]]:
+                interleave_o(g, piece, nc.scalar.copy)
+            for j in range(4):
+                apply_gain(unit)
+                if j == 0:
+                    add_residual(nc.gpsimd, b, 0, POOL)
+                if j < TA:
+                    advance(unit + ACC_BANKS)
+                unit = unit + 1
+            if b == 0:
+                quantize_tokens(5)
+                if not H6:
+                    hidden(6)
+                hidden(7)
+                advance(9)
+                add_residual(nc.vector, b, POOL, 4 * N_TILE)
+                round_y(0, nc.scalar.copy)
+                quantize_tokens(6)
+            else:
+                if b == 1:
+                    quantize_tokens(7)
+                if b >= RL:
+                    transpose_y(b - RL)
+                    copy_y(b - RL, nc.scalar.copy)
+                advance(unit + ACC_BANKS - 1)
+                if b >= QL:
+                    quantize_y(b - QL)
+                add_residual(nc.vector, b, POOL, 4 * N_TILE)
+            for k in range(QA[b], QA[b + 1]):
+                quantize_o(*divmod(2 * PASSES + k, PASSES))
+            advance(unit + ACC_BANKS - 1)
+            store_y(b)
+            if b + 3 < 2 * GROUPS:
+                load_res(batches[b + 3][0], batches[b + 3][1] // 4)
+
+        def pool_round(out, in_):
+            nc.gpsimd.tensor_scalar(out=out, in0=in_, scalar1=1.0, scalar2=0.0, op0=ALU.mult, op1=ALU.add)
 
         last = len(batches) - 1
+        round_y(last - 2, pool_round, 0, 3)
+        round_y(last - 2, nc.scalar.copy, 3, 4)
+        for unit in range(UNITS - 4, UNITS):
+            apply_gain(unit)
         transpose_y(last - 2)
+        for b in (last - 1, last):
+            add_residual(nc.vector, b, 0, 2 * N_TILE)
+            store_y(b)
+        for b in range(last - 1 - QL, last - 2):
+            quantize_y(b)
         copy_y(last - 2, nc.scalar.copy)
-        transpose_y(last - 1)
-        quantize_y(last - 3)
+        round_y(last - 1, nc.scalar.copy)
         round_y(last, nc.vector.tensor_copy)
-        copy_y(last - 1, nc.scalar.copy)
+        transpose_y(last - 1)
         transpose_y(last)
         quantize_y(last - 2)
+        copy_y(last - 1, nc.scalar.copy)
+        copy_y(last, nc.scalar.copy)
         quantize_y(last - 1)
-        copy_y(last, nc.vector.tensor_copy)
         quantize_y(last)
 
         for q in range(4):
-            nc.sync.dma_start(
+            queue = nc.sync if q < 2 else nc.scalar
+            queue.dma_start(
                 out=out_2[:, 4 * q:4 * q + 4, :].bitcast(I32),
                 in_=y_scales[32 * q:32 * q + 16, :].bitcast(I32),
             )

@@ -20,24 +20,28 @@ P = 128
 PACK = 4
 K_PASS = P * PACK
 PASSES = S // K_PASS
+WORDS = S // PACK
 N_TILE = 512
 TILES = M // P
+HALF = TILES // 2
 GROUPS = D // N_TILE
 UNITS = TILES * GROUPS
-HALF = TILES // 2
+QUADRANT = 32
+
 ACC_BANKS = 6
-POOL = 512
-PA = (0, 2, 4, 6, 8, 8, 8, 8)
-RL = 1
-QL = 2
-EARLY = 4
-G1 = 2
-SL = 2
-H6 = 1
-YB = 3
-TA = 1
-QA = (0, 0, 1, 2, 3, 4, 4, 4)
-L_FIRST = 6
+TURN_BANK = 6
+SCALE_BANK = 7
+GAIN_BANK = 5
+EARLY_GROUPS = 2
+ACT_SLOTS = 6
+
+BATCHES = (
+    [(g, t0, HALF) for t0 in (0, HALF) for g in range(EARLY_GROUPS)]
+    + [(g, t0, HALF) for g in range(EARLY_GROUPS, GROUPS) for t0 in (0, HALF)][:-1]
+    + [(GROUPS - 1, HALF, 2), (GROUPS - 1, HALF + 2, 1), (GROUPS - 1, HALF + 3, 1)]
+)
+WHOLE = len(BATCHES) - 3
+UNIT_PLACES = [(b, j) for b, batch in enumerate(BATCHES) for j in range(batch[2])]
 
 
 def tile_slot_combine_shared_expert_g5_kernel(
@@ -56,63 +60,68 @@ def tile_slot_combine_shared_expert_g5_kernel(
         def bank(index, shape, dtype):
             return psum.tile(shape, dtype, name="bank%d" % index, tag="bank%d" % index)
 
+        def sorted_view(row):
+            return row.rearrange("p (w u e) -> p u w e", u=2, e=2)
+
+        def gpsimd_copy(out, in_):
+            nc.gpsimd.tensor_scalar(out=out, in0=in_, scalar1=1.0, scalar2=0.0, op0=ALU.mult, op1=ALU.add)
+
         ident = keep.tile([P, P], F32, align_bytes=64)
         zeros = keep.tile([P, P], BF16, align_bytes=64)
         ones = keep.tile([P, P], BF16, align_bytes=64)
-        rows = keep.tile([P, S + D], BF16, align_bytes=64)
+        rows = keep.tile([P, S + D // 2], BF16, align_bytes=64)
         gain = keep.tile([P, D], BF16, align_bytes=64)
         w_scales = keep.tile([P, PASSES, D], U8, align_bytes=64)
         y_scales = keep.tile([P, M], U8, align_bytes=64)
 
-        tokens, logits, neg_max, exps, sums, inv_sum, c_sorted, c_bank, c_words = {}, {}, {}, {}, {}, {}, {}, {}, {}
-        gates, ups, g_bank, u_bank, silus, h_words = {}, {}, {}, {}, {}, {}
-        t_codes, t_scales, t_bank = {}, {}, {}
+        tokens, ups, neg_max, exps, sums, inv_sum, silus = {}, {}, {}, {}, {}, {}, {}
+        t_bank, t_codes, t_scales = {}, {}, {}
         o_raw, o_words, o_codes, o_scales, w_words = {}, {}, {}, {}, {}
-        res, acc, y, y_sorted, y_bank, y_words, y_codes, gain_bank = {}, {}, {}, {}, {}, {}, {}, {}
+        res, acc, y, y_sorted, y_bank, y_words, y_codes = {}, {}, {}, {}, {}, {}, {}
 
         def load_logits(t):
             tokens[t] = keep.tile([P, S + F], BF16, name="tokens%d" % t, align_bytes=64)
-            logits[t] = tokens[t][:, :S]
-            nc.sync.dma_start(out=logits[t], in_=slot_logits[t * P:(t + 1) * P, :])
+            nc.sync.dma_start(out=tokens[t][:, :S], in_=slot_logits[t * P:(t + 1) * P, :])
 
         def load_gate_up(t):
-            gates[t] = tokens[t][:, S:]
             ups[t] = work.tile([P, F], BF16, name="up_rows", bufs=TILES, align_bytes=64)
-            nc.sync.dma_start(out=gates[t], in_=gate[t * P:(t + 1) * P, :])
+            nc.sync.dma_start(out=tokens[t][:, S:], in_=gate[t * P:(t + 1) * P, :])
             nc.sync.dma_start(out=ups[t][:], in_=up[t * P:(t + 1) * P, :])
 
         def load_o(g, c):
-            o_raw[g, c] = work.tile([P, PACK, N_TILE], BF16, name="o_raw", bufs=4, align_bytes=64)
+            o_raw[g, c] = work.tile(
+                [P, PACK, N_TILE], BF16, name="o_raw", bufs=EARLY_GROUPS * PASSES, align_bytes=64)
             src = slot_rows[c * K_PASS:(c + 1) * K_PASS, g * N_TILE:(g + 1) * N_TILE]
             nc.sync.dma_start(out=o_raw[g, c][:], in_=src.rearrange("(p j) n -> p j n", j=PACK))
 
         def load_w():
-            for q in range(4):
+            for q in range(P // QUADRANT):
                 nc.sync.dma_start(
-                    out=w_scales[32 * q:32 * q + 4, :, :].bitcast(I32),
+                    out=w_scales[QUADRANT * q:QUADRANT * q + 4, :, :].bitcast(I32),
                     in_=down_scales[:, 4 * q:4 * q + 4, :].rearrange("c r n -> r c n").bitcast(I32),
                 )
             for c in range(PASSES):
                 w_words[c] = keep.tile([P, 2 * D], U8, name="w_words%d" % c, align_bytes=64)
                 nc.sync.dma_start(out=w_words[c][:].bitcast(I32), in_=down_words[c].bitcast(I32))
 
-        def load_res(g, half):
-            res[g, half] = work.tile([P, 4, N_TILE], BF16, name="res_rows", bufs=3, align_bytes=64)
-            src = residual[half * 4 * P:(half + 1) * 4 * P, g * N_TILE:(g + 1) * N_TILE]
-            nc.sync.dma_start(out=res[g, half][:], in_=src.rearrange("(j p) n -> p j n", p=P))
+        def load_res(b):
+            g, t0 = BATCHES[b][:2]
+            res[g, t0 // HALF] = work.tile([P, HALF, N_TILE], BF16, name="res_rows", bufs=3, align_bytes=64)
+            src = residual[t0 * P:(t0 + HALF) * P, g * N_TILE:(g + 1) * N_TILE]
+            nc.sync.dma_start(out=res[g, t0 // HALF][:], in_=src.rearrange("(j p) n -> p j n", p=P))
 
         def row_max(t):
             neg_max[t] = work.tile([P, 1], F32, name="neg_max", bufs=TILES)
             nc.vector.tensor_scalar(
-                out=logits[t], in0=logits[t], scalar1=-1.0, scalar2=None,
+                out=tokens[t][:, :S], in0=tokens[t][:, :S], scalar1=-1.0, scalar2=None,
                 op0=ALU.mult, op1=ALU.min, accum_out=neg_max[t][:],
             )
 
         def exponentials(t):
-            exps[t] = work.tile([P, 2, 256, 2], F32, name="act_out", bufs=5, align_bytes=64)
+            exps[t] = work.tile([P, 2, WORDS, 2], F32, name="act_out", bufs=ACT_SLOTS, align_bytes=64)
             sums[t] = work.tile([P, 1], F32, name="exp_sum", bufs=TILES)
             nc.scalar.activation(
-                out=exps[t][:], in_=logits[t].rearrange("p (w u e) -> p u w e", u=2, e=2),
+                out=exps[t][:], in_=sorted_view(tokens[t][:, :S]),
                 func=ACT.Exp, bias=neg_max[t][:], scale=-1.0, accum_out=sums[t][:],
             )
 
@@ -126,12 +135,22 @@ def tile_slot_combine_shared_expert_g5_kernel(
                 in1=scale_bank[:], op0=ALU.mult, op1=ALU.mult,
             )
 
+        def silu(t):
+            silus[t] = work.tile([P, 2, WORDS, 2], F32, name="act_out", bufs=ACT_SLOTS, align_bytes=64)
+            nc.scalar.activation(out=silus[t][:], in_=sorted_view(tokens[t][:, S:]), func=ACT.Silu)
+
+        def gate_up_product(t):
+            nc.vector.tensor_tensor(
+                out=tokens[t][:, S:].rearrange("p (u w e) -> p u w e", u=2, e=2),
+                in0=silus[t][:], in1=sorted_view(ups[t][:]), op=ALU.mult,
+            )
+
         def transpose_tokens(t, part, index):
-            words = tokens[t][:].bitcast(F32)
-            t_bank[t, part] = bank(index, [P, 4, P], F32)
-            for i in range(4):
-                col = (4 * part + i) * P
-                nc.tensor.transpose(t_bank[t, part][:, i, :], words[:, col:col + P], ident[:])
+            pairs = tokens[t][:].bitcast(F32)
+            t_bank[t, part] = bank(index, [P, 2 * PASSES, P], F32)
+            for i in range(2 * PASSES):
+                col = (2 * PASSES * part + i) * P
+                nc.tensor.transpose(t_bank[t, part][:, i, :], pairs[:, col:col + P], ident[:])
 
         def copy_tokens(t, part):
             nc.scalar.copy(
@@ -144,145 +163,145 @@ def tile_slot_combine_shared_expert_g5_kernel(
             t_scales[t] = keep.tile([P, 2 * PASSES * P], U8, name="t_scales%d" % t, align_bytes=64)
             nc.vector.quantize_mx(out=t_codes[t][:].bitcast(FP8X4), scales=t_scales[t][:], in_=tokens[t][:])
 
-        def silu(t):
-            silus[t] = work.tile([P, 2, 256, 2], F32, name="act_out", bufs=5, align_bytes=64)
-            nc.scalar.activation(
-                out=silus[t][:], in_=gates[t].rearrange("p (w u e) -> p u w e", u=2, e=2), func=ACT.Silu,
-            )
+        def hidden(t, next_silu):
+            gate_up_product(t)
+            if next_silu is not None:
+                silu(next_silu)
+            if t < HALF:
+                transpose_tokens(t, 1, TURN_BANK if t % 2 == 0 else (HALF if t == 1 else TURN_BANK + 1))
+            else:
+                transpose_tokens(t, 0, TURN_BANK)
+                transpose_tokens(t, 1, TURN_BANK + 1)
+            if t >= 2:
+                copy_tokens(t, 0)
+            copy_tokens(t, 1)
 
-        def gate_up_product(t):
-            nc.vector.tensor_tensor(
-                out=tokens[t][:, S:].rearrange("p (u w e) -> p u w e", u=2, e=2),
-                in0=silus[t][:], in1=ups[t][:].rearrange("p (w u e) -> p u w e", u=2, e=2), op=ALU.mult,
-            )
+        def new_o_words(g, c):
+            o_words[g, c] = work.tile(
+                [P, N_TILE, PACK], BF16, name="o_words", bufs=EARLY_GROUPS * PASSES, align_bytes=64)
 
-        def interleave_o(g, piece, copy):
-            c, half = divmod(piece, 2)
-            if half == 0:
-                o_words[g, c] = work.tile([P, N_TILE, PACK], BF16, name="o_words", bufs=4, align_bytes=64)
-            cols = slice(half * 256, (half + 1) * 256)
-            copy(
-                out=o_words[g, c][:, cols, :].rearrange("p (n i) t -> p n t i", i=4),
-                in_=o_raw[g, c][:, :, cols].rearrange("p t (n i) -> p n t i", i=4),
-            )
+        def interleave_o_gpsimd(g, c):
+            new_o_words(g, c)
+            gpsimd_copy(o_words[g, c][:], o_raw[g, c][:].rearrange("p t n -> p n t"))
 
-        def interleave_o_early(g, c):
-            o_words[g, c] = work.tile([P, N_TILE, PACK], BF16, name="o_words", bufs=4, align_bytes=64)
-            nc.gpsimd.tensor_scalar(
-                out=o_words[g, c][:], in0=o_raw[g, c][:].rearrange("p t n -> p n t"),
-                scalar1=1.0, scalar2=0.0, op0=ALU.mult, op1=ALU.add,
-            )
+        def interleave_o_scalar(g, c):
+            new_o_words(g, c)
+            for first in (0, N_TILE // 2):
+                cols = slice(first, first + N_TILE // 2)
+                nc.scalar.copy(
+                    out=o_words[g, c][:, cols, :].rearrange("p (n i) t -> p n t i", i=4),
+                    in_=o_raw[g, c][:, :, cols].rearrange("p t (n i) -> p n t i", i=4),
+                )
 
         def quantize_o(g, c):
-            o_codes[g, c] = work.tile([P, N_TILE], U32, name="o_codes", bufs=6, align_bytes=64)
-            o_scales[g, c] = work.tile([P, N_TILE], U8, name="o_scales", bufs=6, align_bytes=64)
+            o_codes[g, c] = work.tile([P, N_TILE], U32, name="o_codes", bufs=3 * PASSES, align_bytes=64)
+            o_scales[g, c] = work.tile([P, N_TILE], U8, name="o_scales", bufs=3 * PASSES, align_bytes=64)
             nc.vector.quantize_mx(
                 out=o_codes[g, c][:].bitcast(FP8X4), scales=o_scales[g, c][:],
                 in_=o_words[g, c][:].rearrange("p n t -> p (n t)"),
             )
 
-        batches = [(0, 0, 4), (1, 0, 4), (0, 4, 4), (1, 4, 4), (2, 0, 4), (2, 4, 4), (3, 0, 4), (3, 4, 2), (3, 6, 2)]
-        units = [(b, j) for b, batch in enumerate(batches) for j in range(batch[2])]
-
         def multiply(unit):
-            b, j = units[unit]
-            g, t = batches[b][0], batches[b][1] + j
+            b, j = UNIT_PLACES[unit]
+            g, t = BATCHES[b][0], BATCHES[b][1] + j
             acc[unit] = bank(unit % ACC_BANKS, [P, N_TILE], F32)
-            cols = slice(g * N_TILE, (g + 1) * N_TILE)
-            passes = []
-            for c in range(PASSES):
-                passes.append((c, o_codes[g, c][:].bitcast(FP8X4), o_scales[g, c][:]))
-            for c in range(PASSES):
-                words = w_words[c][:, 2 * g * N_TILE:2 * (g + 1) * N_TILE]
-                passes.append((PASSES + c, words.bitcast(FP4X4), w_scales[:, c, cols]))
-            for i, (c, rhs, rhs_scale) in enumerate(passes[:1] + passes[2:] + passes[1:2]):
-                tok = slice(c * P, (c + 1) * P)
+            o_passes = [(c, o_codes[g, c][:].bitcast(FP8X4), o_scales[g, c][:]) for c in range(PASSES)]
+            w_passes = [
+                (PASSES + c, w_words[c][:, 2 * g * N_TILE:2 * (g + 1) * N_TILE].bitcast(FP4X4),
+                 w_scales[:, c, g * N_TILE:(g + 1) * N_TILE])
+                for c in range(PASSES)
+            ]
+            passes = o_passes[:1] + w_passes + o_passes[1:]
+            for n, (i, rhs, rhs_scale) in enumerate(passes):
+                tok = slice(i * P, (i + 1) * P)
                 nc.tensor.matmul_mx(
                     out=acc[unit][:], lhsT=t_codes[t][:, tok].bitcast(FP8X4), lhsT_scale=t_scales[t][:, tok],
-                    rhs=rhs, rhs_scale=rhs_scale, start=(i == 0), stop=(i == len(passes) - 1),
+                    rhs=rhs, rhs_scale=rhs_scale, start=(n == 0), stop=(n == len(passes) - 1),
                 )
 
+        def multiply_up_to(limit):
+            for unit in range(len(acc), min(limit + 1, UNITS)):
+                b, j = UNIT_PLACES[unit]
+                g, t0 = BATCHES[b][:2]
+                if unit == len(acc) and t0 + j in t_codes and (g, PASSES - 1) in o_codes:
+                    multiply(unit)
+
+        def batch_view(views, b, width, dtype, name, bufs):
+            if BATCHES[b][1] % HALF == 0:
+                views[b] = work.tile([P, HALF * width], dtype, name=name, bufs=bufs, align_bytes=64)[:]
+            else:
+                views[b] = views[b - 1][:, BATCHES[b - 1][2] * width:]
+
         def apply_gain(unit):
-            b, j = units[unit]
-            g = batches[b][0]
+            b, j = UNIT_PLACES[unit]
+            g = BATCHES[b][0]
             if j == 0:
-                y[b] = work.tile([P, 4 * N_TILE], F32, name="y_rows", bufs=YB, align_bytes=64)
+                batch_view(y, b, N_TILE, F32, "y_rows", 3)
             nc.vector.tensor_tensor(
                 out=y[b][:, j * N_TILE:(j + 1) * N_TILE], in0=acc[unit][:],
                 in1=gain[:, g * N_TILE:(g + 1) * N_TILE], op=ALU.mult,
             )
 
         def add_residual(engine, b, first, end):
-            g, t0, count = batches[b]
-            half, j = divmod(t0, 4)
-            rows_r = res[g, half][:].rearrange("p j n -> p (j n)")
+            g, t0 = BATCHES[b][:2]
+            half, j = divmod(t0, HALF)
+            part = y[b][:, first * N_TILE:end * N_TILE]
+            rows_res = res[g, half][:].rearrange("p j n -> p (j n)")
             engine.tensor_tensor(
-                out=y[b][:, first:end], in0=y[b][:, first:end],
-                in1=rows_r[:, j * N_TILE + first:j * N_TILE + end], op=ALU.add,
-            )
+                out=part, in0=part, in1=rows_res[:, (j + first) * N_TILE:(j + end) * N_TILE], op=ALU.add)
 
-        def store_y(b):
-            g, t0, count = batches[b]
+        def store_y(b, count):
+            g, t0 = BATCHES[b][:2]
             dst = out_0[t0 * P:(t0 + count) * P, g * N_TILE:(g + 1) * N_TILE]
             nc.sync.dma_start(
                 out=dst.rearrange("(j p) n -> p j n", p=P),
                 in_=y[b][:, :count * N_TILE].rearrange("p (j n) -> p j n", n=N_TILE),
             )
 
-        def round_y(b, copy, first=0, end=None):
-            count = batches[b][2]
+        def round_y(copy, b, first, end):
+            count = BATCHES[b][2]
             if first == 0:
-                y_sorted[b] = work.tile([P, 4 * N_TILE], BF16, name="y_sorted", bufs=3, align_bytes=64)
-            part = slice(first * P, (end or count) * P)
+                batch_view(y_sorted, b, N_TILE, BF16, "y_sorted", 3)
+            part = slice(first * P, end * P)
             copy(
                 out=y_sorted[b][:, :count * N_TILE].rearrange("p (u w e) -> p u w e", u=2, e=2)[:, :, part, :],
-                in_=y[b][:, :count * N_TILE].rearrange("p (w u e) -> p u w e", u=2, e=2)[:, :, part, :],
+                in_=sorted_view(y[b][:, :count * N_TILE])[:, :, part, :],
             )
 
         def transpose_y(b):
-            count = batches[b][2]
-            words = y_sorted[b][:].bitcast(F32)
-            for part in range((count + 1) // 2):
-                width = min(2, count)
-                y_bank[b, part] = bank(6 + part if count == 4 else b % 2, [P, 4, P], F32)
+            count = BATCHES[b][2]
+            width = min(2, count)
+            pairs = y_sorted[b].bitcast(F32)
+            for part in range(count // width):
+                y_bank[b, part] = bank(TURN_BANK + part if b < WHOLE else b % 3, [P, 4, P], F32)
                 for u in range(2):
                     for j in range(width):
-                        col = (u * count + 2 * part + j) * P
-                        nc.tensor.transpose(y_bank[b, part][:, u * width + j, :], words[:, col:col + P], ident[:])
+                        col = (u * count + width * part + j) * P
+                        nc.tensor.transpose(y_bank[b, part][:, u * width + j, :], pairs[:, col:col + P], ident[:])
 
-        def copy_y(b, copy):
-            count = batches[b][2]
+        def copy_y(b):
+            count = BATCHES[b][2]
             width = min(2, count)
-            y_words[b] = work.tile([P, 4 * N_TILE], BF16, name="y_words", bufs=4, align_bytes=64)
-            for part in range((count + 1) // 2):
-                dst = y_words[b][:, 2 * part * N_TILE:(2 * part + width) * N_TILE]
-                copy(
+            batch_view(y_words, b, N_TILE, BF16, "y_words", 3)
+            for part in range(count // width):
+                dst = y_words[b][:, width * part * N_TILE:width * (part + 1) * N_TILE]
+                nc.scalar.copy(
                     out=dst.bitcast(F32).rearrange("p (w u) -> p w u", u=2),
                     in_=y_bank[b, part][:, :2 * width, :].rearrange("p (u j) m -> p (j m) u", u=2),
                 )
 
         def quantize_y(b):
-            g, t0, count = batches[b]
-            y_codes[b] = work.tile([P, 4 * P], U32, name="y_codes", bufs=4, align_bytes=64)
-            tok = slice(t0 * P, (t0 + count) * P)
+            g, t0, count = BATCHES[b]
+            batch_view(y_codes, b, P, U32, "y_codes", 4)
             nc.vector.quantize_mx(
-                out=y_codes[b][:, :count * P].bitcast(FP8X4), scales=y_scales[4 * g:P, tok],
+                out=y_codes[b][:, :count * P].bitcast(FP8X4), scales=y_scales[4 * g:P, t0 * P:(t0 + count) * P],
                 in_=y_words[b][:, :count * N_TILE],
             )
+
+        def store_codes(b, count):
+            g, t0 = BATCHES[b][:2]
             dst = out_1[g].rearrange("p m t -> p (m t)").bitcast(I32)
-            nc.sync.dma_start(out=dst[:, tok], in_=y_codes[b][:, :count * P].bitcast(I32))
-
-        def spread_gain(half):
-            gain_bank[half] = bank(6 - half, [P, 2 * N_TILE], BF16)
-            for i in range(2):
-                col = S + (2 * half + i) * N_TILE
-                nc.tensor.matmul(
-                    gain_bank[half][:, i * N_TILE:(i + 1) * N_TILE], lhsT=ones[:], rhs=rows[:, col:col + N_TILE],
-                    start=True, stop=True,
-                )
-
-        def copy_gain(half):
-            nc.scalar.copy(out=gain[:, half * 2 * N_TILE:(half + 1) * 2 * N_TILE], in_=gain_bank[half][:])
+            nc.sync.dma_start(out=dst[:, t0 * P:(t0 + count) * P], in_=y_codes[b][:, :count * P].bitcast(I32))
 
         nc.vector.memset(zeros[:].bitcast(I32), 0)
         nc.vector.memset(rows[:].bitcast(I32), 0)
@@ -290,188 +309,165 @@ def tile_slot_combine_shared_expert_g5_kernel(
         make_identity(nc, ident[:])
         nc.gpsimd.memset(w_scales[:].rearrange("p c n -> p (c n)").bitcast(I32), 0)
 
+        early_o = [(g, c) for g in range(EARLY_GROUPS) for c in range(PASSES)]
+        late_o = [(g, c) for g in range(EARLY_GROUPS, GROUPS) for c in range(PASSES)]
         load_logits(0)
         load_logits(1)
         nc.sync.dma_start(out=rows[0:1, :S], in_=slot_scale.rearrange("(o s) -> o s", o=1))
-        nc.sync.dma_start(out=rows[0:1, S:], in_=layer_scale.rearrange("(o d) -> o d", o=1))
-        for t in range(2, L_FIRST):
-            load_logits(t)
-        load_o(0, 0)
-        for t in range(L_FIRST, TILES):
-            load_logits(t)
-        load_o(0, 1)
-        load_o(1, 0)
+        nc.sync.dma_start(out=rows[0:1, S:], in_=layer_scale[:D // 2].rearrange("(o d) -> o d", o=1))
+        for i in range(3):
+            load_logits(2 * i + 2)
+            load_logits(2 * i + 3)
+            load_o(*early_o[i])
         load_gate_up(0)
-        load_o(1, 1)
-        load_gate_up(1)
-        load_gate_up(2)
-        load_gate_up(3)
-        load_w()
-        for t in range(4, TILES):
+        load_o(*early_o[3])
+        for t in range(1, HALF):
             load_gate_up(t)
-        load_res(0, 0)
-        for g in range(2):
-            for c in range(PASSES):
-                interleave_o_early(g, c)
-        load_o(2, 0)
-        load_res(1, 0)
-        load_o(2, 1)
-        load_res(0, 1)
-        load_o(3, 0)
-        load_o(3, 1)
+        load_w()
+        for t in range(HALF, TILES):
+            load_gate_up(t)
+        load_res(0)
+        for g, c in early_o:
+            interleave_o_gpsimd(g, c)
+        load_o(*late_o[0])
+        load_res(1)
+        load_o(*late_o[1])
+        load_res(2)
+        load_o(*late_o[2])
+        load_o(*late_o[3])
+        nc.sync.dma_start(out=gain[:, D // 2:], in_=layer_scale[D // 2:].partition_broadcast(P))
 
-        scale_bank = bank(7, [P, S], BF16)
-        sorted_scale = rows[:, :S].rearrange("p (w u e) -> p u w e", u=2, e=2)
+        scale_bank = bank(SCALE_BANK, [P, S], BF16)
         for u in range(2):
             nc.tensor.matmul(
-                scale_bank[:, u * N_TILE:(u + 1) * N_TILE], lhsT=ones[:], rhs=sorted_scale[:, u, :, :],
+                scale_bank[:, u * N_TILE:(u + 1) * N_TILE], lhsT=ones[:], rhs=sorted_view(rows[:, :S])[:, u, :, :],
                 start=True, stop=True,
             )
 
-        spread_gain(0)
-
-        for t in range(L_FIRST):
+        for t in range(HALF):
             row_max(t)
-            if t < 4:
-                exponentials(t)
-            if t >= L_FIRST - 2:
-                invert_sum(t - (L_FIRST - 2))
-        for t in range(TILES):
-            if t == 0:
-                copy_gain(0)
-            if t + 4 < TILES and t + 4 < L_FIRST + t:
-                exponentials(t + 4)
-            if t in (4, 5):
-                silu(t - 4)
-            if t == 6:
+            exponentials(t)
+            if t == HALF - 2:
+                invert_sum(0)
+        for t in range(TILES - 1):
+            if t == TILES - 2:
                 copy_tokens(0, 0)
-                silu(2)
+            if t >= HALF:
+                silu(t - HALF)
+            if t == TILES - 2:
                 copy_tokens(1, 0)
             combine_weights(t)
-            if t < EARLY:
+            if t < HALF:
                 transpose_tokens(t, 0, t)
-            if t + L_FIRST < TILES:
-                row_max(t + L_FIRST)
+            if t < 2:
+                row_max(HALF + 2 * t)
+                if t == 0:
+                    invert_sum(1)
+                row_max(HALF + 2 * t + 1)
+            if t < HALF:
+                exponentials(t + HALF)
             if t + 2 < TILES:
                 invert_sum(t + 2)
 
-        def hidden(t):
-            gate_up_product(t)
-            if 1 <= t and t + SL < TILES and t + SL > 3:
-                silu(t + SL)
-            if t < EARLY:
-                transpose_tokens(t, 1, 6 + t % 2)
-                if t >= 2:
-                    copy_tokens(t, 0)
-            else:
-                transpose_tokens(t, 0, 6)
-                transpose_tokens(t, 1, 7)
-                copy_tokens(t, 0)
-            copy_tokens(t, 1)
-            if t == 0:
-                silu(3)
-                spread_gain(1)
-            if t == G1:
-                copy_gain(1)
-
-        hidden(0)
+        hidden(0, None)
+        silu(3)
+        gain_bank = bank(GAIN_BANK, [P, D // 2], BF16)
+        for i in range(2):
+            nc.tensor.matmul(
+                gain_bank[:, i * N_TILE:(i + 1) * N_TILE], lhsT=ones[:],
+                rhs=rows[:, S + i * N_TILE:S + (i + 1) * N_TILE], start=True, stop=True,
+            )
         quantize_o(0, 0)
-        hidden(1)
-        quantize_tokens(0)
+        hidden(1, None)
         quantize_o(0, 1)
+        quantize_tokens(0)
         multiply(0)
-        hidden(2)
-        quantize_o(1, 0)
+        hidden(2, 4)
+        nc.scalar.copy(out=gain[:, :D // 2], in_=gain_bank[:])
         quantize_tokens(1)
         multiply(1)
-        hidden(3)
+        quantize_o(1, 0)
         quantize_o(1, 1)
-        multiply(4)
+        multiply(HALF)
+        combine_weights(TILES - 1)
         quantize_tokens(2)
         multiply(2)
-        hidden(4)
+        hidden(3, 5)
+        multiply(HALF + 1)
+        hidden(4, 6)
         quantize_tokens(3)
         multiply(3)
-        hidden(5)
-        multiply(5)
-        if H6:
-            hidden(6)
+        hidden(5, 7)
+        hidden(6, None)
         quantize_tokens(4)
 
-        def advance(limit):
-            for later in range(len(acc), min(limit + 1, UNITS)):
-                g, t0, count = batches[units[later][0]]
-                if later == len(acc) and t0 + units[later][1] in t_codes and (g, 1) in o_codes:
-                    multiply(later)
-
-        pieces = [(g, piece) for g in (2, 3) for piece in range(4)]
-        unit = 0
-        for b in range(len(batches) - 2):
+        for b in range(WHOLE):
+            first_unit = b * HALF
+            freed = first_unit + HALF - 1 + ACC_BANKS
             if b >= 2:
-                round_y(b - RL, nc.scalar.copy)
-            for g, piece in pieces[PA[b]:PA[b + 1]]:
-                interleave_o(g, piece, nc.scalar.copy)
-            for j in range(4):
+                round_y(nc.scalar.copy, b - 1, 0, HALF)
+            if b < len(late_o):
+                interleave_o_scalar(*late_o[b])
+            apply_gain(first_unit)
+            add_residual(nc.gpsimd, b, 0, 1)
+            multiply_up_to(first_unit + ACC_BANKS)
+            for unit in range(first_unit + 1, first_unit + HALF):
                 apply_gain(unit)
-                if j == 0:
-                    add_residual(nc.gpsimd, b, 0, POOL)
-                if j < TA:
-                    advance(unit + ACC_BANKS)
-                unit = unit + 1
             if b == 0:
                 quantize_tokens(5)
-                if not H6:
-                    hidden(6)
-                hidden(7)
-                advance(9)
-                add_residual(nc.vector, b, POOL, 4 * N_TILE)
-                round_y(0, nc.scalar.copy)
+                hidden(7, None)
+                multiply_up_to(freed)
+                add_residual(nc.vector, b, 1, HALF)
+                round_y(nc.scalar.copy, 0, 0, HALF)
                 quantize_tokens(6)
             else:
                 if b == 1:
                     quantize_tokens(7)
-                if b >= RL:
-                    transpose_y(b - RL)
-                    copy_y(b - RL, nc.scalar.copy)
-                advance(unit + ACC_BANKS - 1)
-                if b >= QL:
-                    quantize_y(b - QL)
-                add_residual(nc.vector, b, POOL, 4 * N_TILE)
-            for k in range(QA[b], QA[b + 1]):
-                quantize_o(*divmod(2 * PASSES + k, PASSES))
-            advance(unit + ACC_BANKS - 1)
-            store_y(b)
-            if b + 3 < 2 * GROUPS:
-                load_res(batches[b + 3][0], batches[b + 3][1] // 4)
+                if b == WHOLE - 1:
+                    multiply_up_to(freed)
+                transpose_y(b - 1)
+                copy_y(b - 1)
+                multiply_up_to(freed)
+                if b >= 2:
+                    quantize_y(b - 2)
+                    store_codes(b - 2, HALF)
+                add_residual(nc.vector, b, 1, HALF)
+            if 1 <= b <= len(late_o):
+                quantize_o(*late_o[b - 1])
+            multiply_up_to(freed)
+            store_y(b, HALF)
+            if b + 3 <= WHOLE:
+                load_res(b + 3)
 
-        def pool_round(out, in_):
-            nc.gpsimd.tensor_scalar(out=out, in0=in_, scalar1=1.0, scalar2=0.0, op0=ALU.mult, op1=ALU.add)
-
-        last = len(batches) - 1
-        round_y(last - 2, pool_round, 0, 3)
-        round_y(last - 2, nc.scalar.copy, 3, 4)
-        for unit in range(UNITS - 4, UNITS):
+        before, pair, single, last = WHOLE - 1, WHOLE, WHOLE + 1, WHOLE + 2
+        round_y(gpsimd_copy, before, 0, HALF - 1)
+        round_y(nc.scalar.copy, before, HALF - 1, HALF)
+        for unit in range(UNITS - HALF, UNITS):
             apply_gain(unit)
-        transpose_y(last - 2)
-        for b in (last - 1, last):
-            add_residual(nc.vector, b, 0, 2 * N_TILE)
-            store_y(b)
-        for b in range(last - 1 - QL, last - 2):
+        transpose_y(before)
+        add_residual(nc.vector, pair, 0, 2)
+        store_y(pair, 2)
+        round_y(nc.scalar.copy, pair, 0, 2)
+        copy_y(before)
+        add_residual(nc.vector, single, 0, 1)
+        add_residual(nc.vector, last, 0, 1)
+        store_y(single, 2)
+        round_y(nc.vector.tensor_copy, single, 0, 1)
+        round_y(nc.vector.tensor_copy, last, 0, 1)
+        for b in (before - 1, before):
             quantize_y(b)
-        copy_y(last - 2, nc.scalar.copy)
-        round_y(last - 1, nc.scalar.copy)
-        round_y(last, nc.vector.tensor_copy)
-        transpose_y(last - 1)
-        transpose_y(last)
-        quantize_y(last - 2)
-        copy_y(last - 1, nc.scalar.copy)
-        copy_y(last, nc.scalar.copy)
-        quantize_y(last - 1)
-        quantize_y(last)
+            store_codes(b, HALF)
+        for b in (pair, single, last):
+            transpose_y(b)
+            copy_y(b)
+            quantize_y(b)
+            if b == single:
+                store_codes(pair, 3)
+        store_codes(last, 1)
 
-        for q in range(4):
+        for q in range(P // QUADRANT):
             queue = nc.sync if q < 2 else nc.scalar
             queue.dma_start(
                 out=out_2[:, 4 * q:4 * q + 4, :].bitcast(I32),
-                in_=y_scales[32 * q:32 * q + 16, :].bitcast(I32),
+                in_=y_scales[QUADRANT * q:QUADRANT * q + 4 * GROUPS, :].bitcast(I32),
             )

from contextlib import ExitStack

import concourse.mybir as mybir
from concourse.masks import make_identity

M, S, F, D = 1024, 1024, 1024, 2048
FLOPS = 2 * M * S * D + 2 * M * F * D

F32 = mybir.dt.float32
BF16 = mybir.dt.bfloat16
I32 = mybir.dt.int32
U32 = mybir.dt.uint32
U8 = mybir.dt.uint8
FP8X4 = mybir.dt.float8_e4m3fn_x4
FP4X4 = mybir.dt.float4_e2m1fn_x4
ALU = mybir.AluOpType
ACT = mybir.ActivationFunctionType

P = 128
PACK = 4
K_PASS = P * PACK
PASSES = S // K_PASS
WORDS = S // PACK
N_TILE = 512
TILES = M // P
HALF = TILES // 2
GROUPS = D // N_TILE
UNITS = TILES * GROUPS
QUADRANT = 32

ACC_BANKS = 6
TURN_BANK = 6
SCALE_BANK = 7
GAIN_BANK = 5
EARLY_GROUPS = 2
ACT_SLOTS = 6

BATCHES = (
    [(g, t0, HALF) for t0 in (0, HALF) for g in range(EARLY_GROUPS)]
    + [(g, t0, HALF) for g in range(EARLY_GROUPS, GROUPS) for t0 in (0, HALF)][:-1]
    + [(GROUPS - 1, HALF, 2), (GROUPS - 1, HALF + 2, 1), (GROUPS - 1, HALF + 3, 1)]
)
WHOLE = len(BATCHES) - 3
UNIT_PLACES = [(b, j) for b, batch in enumerate(BATCHES) for j in range(batch[2])]


def tile_slot_combine_shared_expert_g5_kernel(
    tc, slot_logits, slot_scale, slot_out, gate, up, down_words, down_scales, layer_scale, residual,
    out_0, out_1, out_2,
):
    nc = tc.nc
    slot_rows = slot_out.rearrange("e p d -> (e p) d")

    with ExitStack() as ctx:
        keep = ctx.enter_context(tc.tile_pool(name="keep", bufs=1))
        work = ctx.enter_context(tc.tile_pool(name="work", bufs=3))
        psum = ctx.enter_context(tc.psum_pool(name="psum", bufs=1))
        ctx.enter_context(tc.manual_schedule())

        def bank(index, shape, dtype):
            return psum.tile(shape, dtype, name="bank%d" % index, tag="bank%d" % index)

        def sorted_view(row):
            return row.rearrange("p (w u e) -> p u w e", u=2, e=2)

        def gpsimd_copy(out, in_):
            nc.gpsimd.tensor_scalar(out=out, in0=in_, scalar1=1.0, scalar2=0.0, op0=ALU.mult, op1=ALU.add)

        ident = keep.tile([P, P], F32, align_bytes=64)
        zeros = keep.tile([P, P], BF16, align_bytes=64)
        ones = keep.tile([P, P], BF16, align_bytes=64)
        rows = keep.tile([P, S + D // 2], BF16, align_bytes=64)
        gain = keep.tile([P, D], BF16, align_bytes=64)
        w_scales = keep.tile([P, PASSES, D], U8, align_bytes=64)
        y_scales = keep.tile([P, M], U8, align_bytes=64)

        tokens, ups, neg_max, exps, sums, inv_sum, silus = {}, {}, {}, {}, {}, {}, {}
        t_bank, t_codes, t_scales = {}, {}, {}
        o_raw, o_words, o_codes, o_scales, w_words = {}, {}, {}, {}, {}
        res, acc, y, y_sorted, y_bank, y_words, y_codes = {}, {}, {}, {}, {}, {}, {}

        def load_logits(t):
            tokens[t] = keep.tile([P, S + F], BF16, name="tokens%d" % t, align_bytes=64)
            nc.sync.dma_start(out=tokens[t][:, :S], in_=slot_logits[t * P:(t + 1) * P, :])

        def load_gate_up(t):
            ups[t] = work.tile([P, F], BF16, name="up_rows", bufs=TILES, align_bytes=64)
            nc.sync.dma_start(out=tokens[t][:, S:], in_=gate[t * P:(t + 1) * P, :])
            nc.sync.dma_start(out=ups[t][:], in_=up[t * P:(t + 1) * P, :])

        def load_o(g, c):
            o_raw[g, c] = work.tile(
                [P, PACK, N_TILE], BF16, name="o_raw", bufs=EARLY_GROUPS * PASSES, align_bytes=64)
            src = slot_rows[c * K_PASS:(c + 1) * K_PASS, g * N_TILE:(g + 1) * N_TILE]
            nc.sync.dma_start(out=o_raw[g, c][:], in_=src.rearrange("(p j) n -> p j n", j=PACK))

        def load_w():
            for q in range(P // QUADRANT):
                nc.sync.dma_start(
                    out=w_scales[QUADRANT * q:QUADRANT * q + 4, :, :].bitcast(I32),
                    in_=down_scales[:, 4 * q:4 * q + 4, :].rearrange("c r n -> r c n").bitcast(I32),
                )
            for c in range(PASSES):
                w_words[c] = keep.tile([P, 2 * D], U8, name="w_words%d" % c, align_bytes=64)
                nc.sync.dma_start(out=w_words[c][:].bitcast(I32), in_=down_words[c].bitcast(I32))

        def load_res(b):
            g, t0 = BATCHES[b][:2]
            res[g, t0 // HALF] = work.tile([P, HALF, N_TILE], BF16, name="res_rows", bufs=3, align_bytes=64)
            src = residual[t0 * P:(t0 + HALF) * P, g * N_TILE:(g + 1) * N_TILE]
            nc.sync.dma_start(out=res[g, t0 // HALF][:], in_=src.rearrange("(j p) n -> p j n", p=P))

        def row_max(t):
            neg_max[t] = work.tile([P, 1], F32, name="neg_max", bufs=TILES)
            nc.vector.tensor_scalar(
                out=tokens[t][:, :S], in0=tokens[t][:, :S], scalar1=-1.0, scalar2=None,
                op0=ALU.mult, op1=ALU.min, accum_out=neg_max[t][:],
            )

        def exponentials(t):
            exps[t] = work.tile([P, 2, WORDS, 2], F32, name="act_out", bufs=ACT_SLOTS, align_bytes=64)
            sums[t] = work.tile([P, 1], F32, name="exp_sum", bufs=TILES)
            nc.scalar.activation(
                out=exps[t][:], in_=sorted_view(tokens[t][:, :S]),
                func=ACT.Exp, bias=neg_max[t][:], scale=-1.0, accum_out=sums[t][:],
            )

        def invert_sum(t):
            inv_sum[t] = work.tile([P, 1], F32, name="inv_sum", bufs=TILES)
            nc.vector.reciprocal(out=inv_sum[t][:], in_=sums[t][:])

        def combine_weights(t):
            nc.vector.scalar_tensor_tensor(
                out=tokens[t][:, :S], in0=exps[t][:].rearrange("p u w e -> p (u w e)"), scalar=inv_sum[t][:],
                in1=scale_bank[:], op0=ALU.mult, op1=ALU.mult,
            )

        def silu(t):
            silus[t] = work.tile([P, 2, WORDS, 2], F32, name="act_out", bufs=ACT_SLOTS, align_bytes=64)
            nc.scalar.activation(out=silus[t][:], in_=sorted_view(tokens[t][:, S:]), func=ACT.Silu)

        def gate_up_product(t):
            nc.vector.tensor_tensor(
                out=tokens[t][:, S:].rearrange("p (u w e) -> p u w e", u=2, e=2),
                in0=silus[t][:], in1=sorted_view(ups[t][:]), op=ALU.mult,
            )

        def transpose_tokens(t, part, index):
            pairs = tokens[t][:].bitcast(F32)
            t_bank[t, part] = bank(index, [P, 2 * PASSES, P], F32)
            for i in range(2 * PASSES):
                col = (2 * PASSES * part + i) * P
                nc.tensor.transpose(t_bank[t, part][:, i, :], pairs[:, col:col + P], ident[:])

        def copy_tokens(t, part):
            nc.scalar.copy(
                out=tokens[t][:, part * S:(part + 1) * S].bitcast(F32).rearrange("p (w u) -> p w u", u=2),
                in_=t_bank[t, part][:].rearrange("p (u c) m -> p (c m) u", u=2),
            )

        def quantize_tokens(t):
            t_codes[t] = keep.tile([P, 2 * PASSES * P], U32, name="t_codes%d" % t, align_bytes=64)
            t_scales[t] = keep.tile([P, 2 * PASSES * P], U8, name="t_scales%d" % t, align_bytes=64)
            nc.vector.quantize_mx(out=t_codes[t][:].bitcast(FP8X4), scales=t_scales[t][:], in_=tokens[t][:])

        def hidden(t, next_silu):
            gate_up_product(t)
            if next_silu is not None:
                silu(next_silu)
            if t < HALF:
                transpose_tokens(t, 1, TURN_BANK if t % 2 == 0 else (HALF if t == 1 else TURN_BANK + 1))
            else:
                transpose_tokens(t, 0, TURN_BANK)
                transpose_tokens(t, 1, TURN_BANK + 1)
            if t >= 2:
                copy_tokens(t, 0)
            copy_tokens(t, 1)

        def new_o_words(g, c):
            o_words[g, c] = work.tile(
                [P, N_TILE, PACK], BF16, name="o_words", bufs=EARLY_GROUPS * PASSES, align_bytes=64)

        def interleave_o_gpsimd(g, c):
            new_o_words(g, c)
            gpsimd_copy(o_words[g, c][:], o_raw[g, c][:].rearrange("p t n -> p n t"))

        def interleave_o_scalar(g, c):
            new_o_words(g, c)
            for first in (0, N_TILE // 2):
                cols = slice(first, first + N_TILE // 2)
                nc.scalar.copy(
                    out=o_words[g, c][:, cols, :].rearrange("p (n i) t -> p n t i", i=4),
                    in_=o_raw[g, c][:, :, cols].rearrange("p t (n i) -> p n t i", i=4),
                )

        def quantize_o(g, c):
            o_codes[g, c] = work.tile([P, N_TILE], U32, name="o_codes", bufs=3 * PASSES, align_bytes=64)
            o_scales[g, c] = work.tile([P, N_TILE], U8, name="o_scales", bufs=3 * PASSES, align_bytes=64)
            nc.vector.quantize_mx(
                out=o_codes[g, c][:].bitcast(FP8X4), scales=o_scales[g, c][:],
                in_=o_words[g, c][:].rearrange("p n t -> p (n t)"),
            )

        def multiply(unit):
            b, j = UNIT_PLACES[unit]
            g, t = BATCHES[b][0], BATCHES[b][1] + j
            acc[unit] = bank(unit % ACC_BANKS, [P, N_TILE], F32)
            o_passes = [(c, o_codes[g, c][:].bitcast(FP8X4), o_scales[g, c][:]) for c in range(PASSES)]
            w_passes = [
                (PASSES + c, w_words[c][:, 2 * g * N_TILE:2 * (g + 1) * N_TILE].bitcast(FP4X4),
                 w_scales[:, c, g * N_TILE:(g + 1) * N_TILE])
                for c in range(PASSES)
            ]
            passes = o_passes[:1] + w_passes + o_passes[1:]
            for n, (i, rhs, rhs_scale) in enumerate(passes):
                tok = slice(i * P, (i + 1) * P)
                nc.tensor.matmul_mx(
                    out=acc[unit][:], lhsT=t_codes[t][:, tok].bitcast(FP8X4), lhsT_scale=t_scales[t][:, tok],
                    rhs=rhs, rhs_scale=rhs_scale, start=(n == 0), stop=(n == len(passes) - 1),
                )

        def multiply_up_to(limit):
            for unit in range(len(acc), min(limit + 1, UNITS)):
                b, j = UNIT_PLACES[unit]
                g, t0 = BATCHES[b][:2]
                if unit == len(acc) and t0 + j in t_codes and (g, PASSES - 1) in o_codes:
                    multiply(unit)

        def batch_view(views, b, width, dtype, name, bufs):
            if BATCHES[b][1] % HALF == 0:
                views[b] = work.tile([P, HALF * width], dtype, name=name, bufs=bufs, align_bytes=64)[:]
            else:
                views[b] = views[b - 1][:, BATCHES[b - 1][2] * width:]

        def apply_gain(unit):
            b, j = UNIT_PLACES[unit]
            g = BATCHES[b][0]
            if j == 0:
                batch_view(y, b, N_TILE, F32, "y_rows", 3)
            nc.vector.tensor_tensor(
                out=y[b][:, j * N_TILE:(j + 1) * N_TILE], in0=acc[unit][:],
                in1=gain[:, g * N_TILE:(g + 1) * N_TILE], op=ALU.mult,
            )

        def add_residual(engine, b, first, end):
            g, t0 = BATCHES[b][:2]
            half, j = divmod(t0, HALF)
            part = y[b][:, first * N_TILE:end * N_TILE]
            rows_res = res[g, half][:].rearrange("p j n -> p (j n)")
            engine.tensor_tensor(
                out=part, in0=part, in1=rows_res[:, (j + first) * N_TILE:(j + end) * N_TILE], op=ALU.add)

        def store_y(b, count):
            g, t0 = BATCHES[b][:2]
            dst = out_0[t0 * P:(t0 + count) * P, g * N_TILE:(g + 1) * N_TILE]
            nc.sync.dma_start(
                out=dst.rearrange("(j p) n -> p j n", p=P),
                in_=y[b][:, :count * N_TILE].rearrange("p (j n) -> p j n", n=N_TILE),
            )

        def round_y(copy, b, first, end):
            count = BATCHES[b][2]
            if first == 0:
                batch_view(y_sorted, b, N_TILE, BF16, "y_sorted", 3)
            part = slice(first * P, end * P)
            copy(
                out=y_sorted[b][:, :count * N_TILE].rearrange("p (u w e) -> p u w e", u=2, e=2)[:, :, part, :],
                in_=sorted_view(y[b][:, :count * N_TILE])[:, :, part, :],
            )

        def transpose_y(b):
            count = BATCHES[b][2]
            width = min(2, count)
            pairs = y_sorted[b].bitcast(F32)
            for part in range(count // width):
                y_bank[b, part] = bank(TURN_BANK + part if b < WHOLE else b % 3, [P, 4, P], F32)
                for u in range(2):
                    for j in range(width):
                        col = (u * count + width * part + j) * P
                        nc.tensor.transpose(y_bank[b, part][:, u * width + j, :], pairs[:, col:col + P], ident[:])

        def copy_y(b):
            count = BATCHES[b][2]
            width = min(2, count)
            batch_view(y_words, b, N_TILE, BF16, "y_words", 3)
            for part in range(count // width):
                dst = y_words[b][:, width * part * N_TILE:width * (part + 1) * N_TILE]
                nc.scalar.copy(
                    out=dst.bitcast(F32).rearrange("p (w u) -> p w u", u=2),
                    in_=y_bank[b, part][:, :2 * width, :].rearrange("p (u j) m -> p (j m) u", u=2),
                )

        def quantize_y(b):
            g, t0, count = BATCHES[b]
            batch_view(y_codes, b, P, U32, "y_codes", 4)
            nc.vector.quantize_mx(
                out=y_codes[b][:, :count * P].bitcast(FP8X4), scales=y_scales[4 * g:P, t0 * P:(t0 + count) * P],
                in_=y_words[b][:, :count * N_TILE],
            )

        def store_codes(b, count):
            g, t0 = BATCHES[b][:2]
            dst = out_1[g].rearrange("p m t -> p (m t)").bitcast(I32)
            nc.sync.dma_start(out=dst[:, t0 * P:(t0 + count) * P], in_=y_codes[b][:, :count * P].bitcast(I32))

        nc.vector.memset(zeros[:].bitcast(I32), 0)
        nc.vector.memset(rows[:].bitcast(I32), 0)
        nc.scalar.activation(out=ones[:], in_=zeros[:], func=ACT.Exp)
        make_identity(nc, ident[:])
        nc.gpsimd.memset(w_scales[:].rearrange("p c n -> p (c n)").bitcast(I32), 0)

        early_o = [(g, c) for g in range(EARLY_GROUPS) for c in range(PASSES)]
        late_o = [(g, c) for g in range(EARLY_GROUPS, GROUPS) for c in range(PASSES)]
        load_logits(0)
        load_logits(1)
        nc.sync.dma_start(out=rows[0:1, :S], in_=slot_scale.rearrange("(o s) -> o s", o=1))
        nc.sync.dma_start(out=rows[0:1, S:], in_=layer_scale[:D // 2].rearrange("(o d) -> o d", o=1))
        for i in range(3):
            load_logits(2 * i + 2)
            load_logits(2 * i + 3)
            load_o(*early_o[i])
        load_gate_up(0)
        load_o(*early_o[3])
        for t in range(1, HALF):
            load_gate_up(t)
        load_w()
        for t in range(HALF, TILES):
            load_gate_up(t)
        load_res(0)
        for g, c in early_o:
            interleave_o_gpsimd(g, c)
        load_o(*late_o[0])
        load_res(1)
        load_o(*late_o[1])
        load_res(2)
        load_o(*late_o[2])
        load_o(*late_o[3])
        nc.sync.dma_start(out=gain[:, D // 2:], in_=layer_scale[D // 2:].partition_broadcast(P))

        scale_bank = bank(SCALE_BANK, [P, S], BF16)
        for u in range(2):
            nc.tensor.matmul(
                scale_bank[:, u * N_TILE:(u + 1) * N_TILE], lhsT=ones[:], rhs=sorted_view(rows[:, :S])[:, u, :, :],
                start=True, stop=True,
            )

        for t in range(HALF):
            row_max(t)
            exponentials(t)
            if t == HALF - 2:
                invert_sum(0)
        for t in range(TILES - 1):
            if t == TILES - 2:
                copy_tokens(0, 0)
            if t >= HALF:
                silu(t - HALF)
            if t == TILES - 2:
                copy_tokens(1, 0)
            combine_weights(t)
            if t < HALF:
                transpose_tokens(t, 0, t)
            if t < 2:
                row_max(HALF + 2 * t)
                if t == 0:
                    invert_sum(1)
                row_max(HALF + 2 * t + 1)
            if t < HALF:
                exponentials(t + HALF)
            if t + 2 < TILES:
                invert_sum(t + 2)

        hidden(0, None)
        silu(3)
        gain_bank = bank(GAIN_BANK, [P, D // 2], BF16)
        for i in range(2):
            nc.tensor.matmul(
                gain_bank[:, i * N_TILE:(i + 1) * N_TILE], lhsT=ones[:],
                rhs=rows[:, S + i * N_TILE:S + (i + 1) * N_TILE], start=True, stop=True,
            )
        quantize_o(0, 0)
        hidden(1, None)
        quantize_o(0, 1)
        quantize_tokens(0)
        multiply(0)
        hidden(2, 4)
        nc.scalar.copy(out=gain[:, :D // 2], in_=gain_bank[:])
        quantize_tokens(1)
        multiply(1)
        quantize_o(1, 0)
        quantize_o(1, 1)
        multiply(HALF)
        combine_weights(TILES - 1)
        quantize_tokens(2)
        multiply(2)
        hidden(3, 5)
        multiply(HALF + 1)
        hidden(4, 6)
        quantize_tokens(3)
        multiply(3)
        hidden(5, 7)
        hidden(6, None)
        quantize_tokens(4)

        for b in range(WHOLE):
            first_unit = b * HALF
            freed = first_unit + HALF - 1 + ACC_BANKS
            if b >= 2:
                round_y(nc.scalar.copy, b - 1, 0, HALF)
            if b < len(late_o):
                interleave_o_scalar(*late_o[b])
            apply_gain(first_unit)
            add_residual(nc.gpsimd, b, 0, 1)
            multiply_up_to(first_unit + ACC_BANKS)
            for unit in range(first_unit + 1, first_unit + HALF):
                apply_gain(unit)
            if b == 0:
                quantize_tokens(5)
                hidden(7, None)
                multiply_up_to(freed)
                add_residual(nc.vector, b, 1, HALF)
                round_y(nc.scalar.copy, 0, 0, HALF)
                quantize_tokens(6)
            else:
                if b == 1:
                    quantize_tokens(7)
                if b == WHOLE - 1:
                    multiply_up_to(freed)
                transpose_y(b - 1)
                copy_y(b - 1)
                multiply_up_to(freed)
                if b >= 2:
                    quantize_y(b - 2)
                    store_codes(b - 2, HALF)
                add_residual(nc.vector, b, 1, HALF)
            if 1 <= b <= len(late_o):
                quantize_o(*late_o[b - 1])
            multiply_up_to(freed)
            store_y(b, HALF)
            if b + 3 <= WHOLE:
                load_res(b + 3)

        before, pair, single, last = WHOLE - 1, WHOLE, WHOLE + 1, WHOLE + 2
        round_y(gpsimd_copy, before, 0, HALF - 1)
        round_y(nc.scalar.copy, before, HALF - 1, HALF)
        for unit in range(UNITS - HALF, UNITS):
            apply_gain(unit)
        transpose_y(before)
        add_residual(nc.vector, pair, 0, 2)
        store_y(pair, 2)
        round_y(nc.scalar.copy, pair, 0, 2)
        copy_y(before)
        add_residual(nc.vector, single, 0, 1)
        add_residual(nc.vector, last, 0, 1)
        store_y(single, 2)
        round_y(nc.vector.tensor_copy, single, 0, 1)
        round_y(nc.vector.tensor_copy, last, 0, 1)
        for b in (before - 1, before):
            quantize_y(b)
            store_codes(b, HALF)
        for b in (pair, single, last):
            transpose_y(b)
            copy_y(b)
            quantize_y(b)
            if b == single:
                store_codes(pair, 3)
        store_codes(last, 1)

        for q in range(P // QUADRANT):
            queue = nc.sync if q < 2 else nc.scalar
            queue.dma_start(
                out=out_2[:, 4 * q:4 * q + 4, :].bitcast(I32),
                in_=y_scales[QUADRANT * q:QUADRANT * q + 4 * GROUPS, :].bitcast(I32),
            )
